import numpy as np
import ml_dtypes


def mxq(x, axis, fmt="e4m3"):
    dtype, down = {"e4m3": (ml_dtypes.float8_e4m3fn, 7), "e5m2": (ml_dtypes.float8_e5m2, 14)}[fmt]
    v = np.moveaxis(np.asarray(x, np.float32).astype(ml_dtypes.bfloat16).astype(np.float64), axis, -1)
    blocks = v.reshape(v.shape[:-1] + (-1, 32))
    amax = np.abs(blocks).max(-1, keepdims=True)
    byte = np.maximum(np.where(amax > 0, np.frexp(amax)[1] - 1 + 127, 0) - down, 1)
    scale = np.exp2(byte - 127.0)
    codes = (blocks / scale).astype(np.float32).astype(dtype).astype(np.float64)
    return np.moveaxis((codes * scale).reshape(v.shape), -1, axis)


WIDE = False


def mx_kscale(k):
    if not WIDE:
        return np.ones(k)
    levels = np.array([18, -18])
    if k % 512:
        return np.exp2(np.random.permutation(np.resize(levels, k // 32))).repeat(32)
    a = np.empty((k // 512, 16))
    for p in range(k // 512):
        a[p, :8] = np.random.permutation(np.resize(levels, 8))
        for g in range(8):
            far = levels[np.abs(levels - a[p, g]) >= 10]
            a[p, g + 8] = far[np.random.randint(len(far))]
    return np.exp2(a.ravel()).repeat(32)


def f64(x):
    return np.asarray(x).astype(np.float64)


def striped(idx):
    return np.tile(np.asarray(idx).reshape(-1, 16).T, (8, 1)).astype(np.uint16)


def unstriped(offs):
    return offs[:16].T.reshape(-1).astype(np.int64)

def planes(y):
    n, m = y.shape
    v = y.astype(np.float32).astype(ml_dtypes.bfloat16).astype(np.float64).reshape(n // 32, 32, m)
    top = np.abs(v).max(1)
    byte = np.clip(np.where(top > 0, np.frexp(top)[1] - 1 + 127 - 7, 1), 1, 254)
    codes = (v * np.exp2(127.0 - byte)[:, None, :]).reshape(n, m).astype(np.float32).astype(ml_dtypes.float8_e4m3fn).view(np.uint8)
    words = codes.reshape(n // 512, 128, 4, m).transpose(0, 1, 3, 2)
    return np.ascontiguousarray(words), np.ascontiguousarray(byte.astype(np.uint8).reshape(n // 512, 16, m))


B, N, T, D, DV, R = 1, 512, 2048, 512, 512, 512


def setup_inputs():
    n = np.random.standard_normal
    idx = np.random.permutation(T)[:B * N]
    s = mx_kscale(D)[:, None]
    z = mx_kscale(R)[:, None]
    v = mx_kscale(DV)[:, None]
    q = n((B, D, R))
    do = n((B, DV, R))
    return {
        "qT": (q * s).astype(np.float32),
        "kT": (n((D, T)) * (1.00 / np.sqrt(D)) / s).astype(np.float32),
        "vT": (n((DV, T)) / np.sqrt(DV) / v).astype(np.float32),
        "doT": (do * v).astype(np.float32),
        "rw": (np.random.uniform(0.5, 1.5, (B, R, 1)) * 1.0 / np.sqrt(R) * z).astype(np.float32),
        "qm": (q.transpose(0, 2, 1) / z).astype(np.float32),
        "offs": striped(idx),
    }


def reference(qT, kT, vT, doT, rw, qm, offs):
    idx = unstriped(offs)
    pick = lambda x: x[:, idx].reshape(x.shape[0], B, N).transpose(1, 0, 2)
    a = mxq(f64(qT), 1, "e4m3").transpose(0, 2, 1) @ mxq(pick(f64(kT)), 1, "e4m3")
    p = np.tanh(a)
    dp = mxq(f64(doT), 1, "e5m2").transpose(0, 2, 1) @ mxq(pick(f64(vT)), 1, "e4m3")
    ds = f64(rw) * dp * (1.0 - p * p)
    dk = mxq(f64(qm), 1, "e4m3").transpose(0, 2, 1) @ mxq(ds, 1, "e5m2")
    gk = np.zeros((D, T))
    gk[:, idx] = dk.transpose(1, 0, 2).reshape(D, B * N)
    out_0 = gk
    return (out_0,) + planes(out_0)

@@ -1,0 +1,197 @@
+from contextlib import ExitStack
+
+import concourse.mybir as mybir
+
+N, T, D, DV, R = 512, 2048, 512, 512, 512
+FLOPS = 2 * N * R * (D + DV + D)
+
+F32 = mybir.dt.float32
+BF16 = mybir.dt.bfloat16
+I32 = mybir.dt.int32
+U32 = mybir.dt.uint32
+U16 = mybir.dt.uint16
+U8 = mybir.dt.uint8
+E4M3 = mybir.dt.float8_e4m3fn_x4
+E5M2 = mybir.dt.float8_e5m2_x4
+ACT = mybir.ActivationFunctionType
+ALU = mybir.AluOpType
+
+P = 128
+PACK = 4
+CHUNK = 512
+CHUNKS = T // CHUNK
+DEAL_SPLIT = 64
+WEAVE_SPLIT = 352
+
+
+def tile_attend_gat_pl_tnh_k_kernel(tc, qT, kT, vT, doT, rw, qm, offs, out_0, out_1, out_2):
+    nc = tc.nc
+    with ExitStack() as ctx:
+        keep = ctx.enter_context(tc.tile_pool(name="keep", bufs=1))
+        big = ctx.enter_context(tc.tile_pool(name="big", bufs=4))
+        psum = ctx.enter_context(tc.psum_pool(name="psum", bufs=1))
+
+        def load_pool(src, tag, offsets=None):
+            planes = []
+            rows = src.rearrange("(p j) t -> p j t", j=PACK)
+            for j in range(PACK):
+                plane = big.tile([P, T], F32, name=tag + str(j), tag=tag, align_bytes=64)
+                nc.sync.dma_start(out=plane[:], in_=rows[:, j, :])
+                planes.append(plane)
+                if j == 0 and offsets is not None:
+                    nc.sync.dma_start(offsets[:], offs)
+            return planes
+
+        def load_square(src, name):
+            raw = keep.tile([P, PACK, 512], F32, name=name, align_bytes=64)
+            nc.sync.dma_start(out=raw[:], in_=src[0].rearrange("(p j) w -> p j w", j=PACK))
+            return raw
+
+        def mx_tiles(name, width):
+            codes = keep.tile([P, width], U32, name=name + "_codes", align_bytes=64)
+            scales = keep.tile([P, width], U8, name=name + "_scales", align_bytes=64)
+            return codes, scales
+
+        def deal(raw, name, split):
+            dealt = keep.tile([P, PACK * 512], BF16, name=name, align_bytes=64)
+            dst = dealt[:].rearrange("p (t m j) -> p m j t", t=PACK, j=PACK)
+            src = raw[:].rearrange("p j (m t) -> p m j t", t=PACK)
+            if split > 0:
+                nc.vector.tensor_copy(out=dst[:, :split], in_=src[:, :split])
+            nc.scalar.copy(out=dst[:, split:], in_=src[:, split:])
+            return dealt
+
+        def quantize(src, codes, scales, fmt, first, count):
+            nc.vector.quantize_mx(
+                out=codes[:, first : first + count].bitcast(fmt),
+                scales=scales[:, first : first + count],
+                in_=src[:, PACK * first : PACK * (first + count)],
+            )
+
+        def gather(planes, name):
+            picked = keep.tile([P, N * PACK], BF16, name=name, align_bytes=64)
+            lanes = picked[:].rearrange("p (n j) -> p n j", j=PACK)
+            for j in range(PACK):
+                nc.vector.tensor_copy(out=lanes[:, :, j], in_=planes[j][:].indirect(offsets[:]))
+            return picked
+
+        def product(bank, stat, stat_fmt, t, mov, mov_fmt):
+            cols = slice(t * P, (t + 1) * P)
+            nc.tensor.matmul_mx(
+                out=bank[:],
+                lhsT=stat[0][:, cols].bitcast(stat_fmt),
+                lhsT_scale=stat[1][:, cols],
+                rhs=mov[0][:].bitcast(mov_fmt),
+                rhs_scale=mov[1][:],
+                start=True,
+                stop=True,
+            )
+
+        offsets = keep.tile([P, N // 16], U16, name="offsets")
+        k_planes = load_pool(kT, "kpool", offsets)
+        q_raw = load_square(qT, "q_raw")
+        gate = keep.tile([P, PACK], F32, name="gate")
+        nc.sync.dma_start(out=gate[:], in_=rw[0].rearrange("(p j) o -> p (j o)", j=PACK))
+        v_planes = load_pool(vT, "vpool")
+        do_raw = load_square(doT, "do_raw")
+        qm_raw = load_square(qm, "qm_raw")
+
+        windows = []
+        for j in range(PACK):
+            window = keep.tile([P, T], F32, name="window" + str(j), align_bytes=64)
+            nc.gpsimd.memset(window[:], 0.0)
+            windows.append(window)
+
+        k_mx = mx_tiles("k", N)
+        quantize(gather(k_planes, "k_picked"), *k_mx, E4M3, 0, N)
+        q_mx = mx_tiles("q", R)
+        quantize(deal(q_raw, "q_dealt", DEAL_SPLIT), *q_mx, E4M3, 0, R)
+        neg_gate = keep.tile([P, PACK], F32, name="neg_gate")
+        nc.vector.tensor_scalar(out=neg_gate[:], in0=gate[:], scalar1=-1.0, scalar2=None, op0=ALU.mult)
+        slopes = []
+        for t in range(PACK):
+            bank = psum.tile([P, N], F32, name="score" + str(t), tag="bank" + str(t))
+            product(bank, q_mx, E4M3, t, k_mx, E4M3)
+            weight = keep.tile([P, N], F32, name="weight" + str(t), tag="weight", bufs=2)
+            nc.scalar.activation(out=weight[:], in_=bank[:], func=ACT.Tanh)
+            square = keep.tile([P, N], F32, name="square" + str(t), tag="square", bufs=2)
+            nc.scalar.activation(out=square[:], in_=weight[:], func=ACT.Square)
+            slope = keep.tile([P, N], F32, name="slope" + str(t))
+            nc.vector.tensor_scalar(
+                out=slope[:], in0=square[:], scalar1=neg_gate[:, t : t + 1], scalar2=gate[:, t : t + 1],
+                op0=ALU.mult, op1=ALU.add,
+            )
+            slopes.append(slope)
+
+        v_mx = mx_tiles("v", N)
+        quantize(gather(v_planes, "v_picked"), *v_mx, E4M3, 0, N)
+        do_mx = mx_tiles("do", R)
+        do_dealt = deal(do_raw, "do_dealt", DEAL_SPLIT)
+        for t in range(PACK):
+            quantize(do_dealt, *do_mx, E5M2, t * P, P)
+        ds_rows = keep.tile([P, PACK, N], BF16, name="ds_rows", align_bytes=64)
+        for t in range(PACK):
+            bank = psum.tile([P, N], F32, name="dp" + str(t), tag="bank" + str(PACK + t))
+            product(bank, do_mx, E5M2, t, v_mx, E4M3)
+            nc.vector.tensor_tensor(out=ds_rows[:, t, :], in0=bank[:], in1=slopes[t][:], op=ALU.mult)
+        ds_woven = keep.tile([P, N * PACK], BF16, name="ds_woven", align_bytes=64)
+        dst = ds_woven[:].rearrange("p (c i t) -> p c t i", i=4, t=PACK)
+        src = ds_rows[:].rearrange("p t (c i) -> p c t i", i=4)
+        nc.vector.tensor_copy(out=dst[:, : WEAVE_SPLIT // 4], in_=src[:, : WEAVE_SPLIT // 4])
+        nc.scalar.copy(out=dst[:, WEAVE_SPLIT // 4 :], in_=src[:, WEAVE_SPLIT // 4 :])
+        ds_mx = mx_tiles("ds", N)
+        quantize(ds_woven, *ds_mx, E5M2, 0, N)
+
+        qm_mx = mx_tiles("qm", D)
+        qm_dealt = deal(qm_raw, "qm_dealt", 0)
+        for j in range(PACK):
+            quantize(qm_dealt, *qm_mx, E4M3, j * P, P)
+        grads = []
+
+        def pieces(j):
+            return ((0, N // 2), (N // 2, N)) if j == 0 else ((0, N),)
+
+        for j in range(PACK):
+            bank = psum.tile([P, N], F32, name="dk" + str(j), tag="bank" + str(j))
+            product(bank, qm_mx, E4M3, j, ds_mx, E5M2)
+            grad = keep.tile([P, N], F32, name="grad" + str(j))
+            for lo, hi in pieces(j):
+                nc.scalar.copy(out=grad[:, lo:hi], in_=bank[:, lo:hi])
+            grads.append(grad)
+
+        pairs = [big.tile([P, 2, CHUNK, 2], BF16, name="pairs" + str(c), tag="kpool", align_bytes=64) for c in range(CHUNKS)]
+        out_rows = out_0.rearrange("(p j) t -> p j t", j=PACK)
+        for j in range(PACK):
+            for lo, hi in pieces(j):
+                nc.vector.tensor_copy(out=windows[j][:].indirect(offsets[:, lo // 16 : hi // 16]), in_=grads[j][:, lo:hi])
+            nc.sync.dma_start(out=out_rows[:, j, :], in_=windows[j][:])
+            for c in range(CHUNKS):
+                dst = pairs[c][:, j // 2, :, j % 2]
+                src = windows[j][:, c * CHUNK : (c + 1) * CHUNK]
+                if j == PACK - 1 and c == 0:
+                    nc.vector.tensor_copy(out=dst, in_=src)
+                elif j == PACK - 2 and c == 0:
+                    nc.scalar.copy(out=pairs[c][:, j // 2], in_=src.unsqueeze(2).to_broadcast([P, CHUNK, 2]))
+                else:
+                    nc.scalar.copy(out=dst, in_=src)
+
+        out_scales = keep.tile([P, CHUNK], U8, name="out_scales", align_bytes=64)
+        words = out_1[0].rearrange("p t l -> p (t l)").bitcast(I32)
+        for c in range(CHUNKS):
+            cols = slice(c * CHUNK, (c + 1) * CHUNK)
+            woven = big.tile([P, CHUNK * PACK], BF16, name="woven" + str(c), tag="vpool", align_bytes=64)
+            dst = woven[:].bitcast(F32).rearrange("p (g i u) -> p g u i", i=4, u=2)
+            src = pairs[c][:].rearrange("p u n e -> p u (n e)").bitcast(F32).rearrange("p u (g i) -> p g u i", i=4)
+            if c == CHUNKS - 1:
+                nc.scalar.copy(out=dst, in_=src)
+            else:
+                nc.vector.tensor_copy(out=dst, in_=src)
+            out_codes = keep.tile([P, CHUNK], U32, name="out_codes" + str(c), align_bytes=64)
+            nc.vector.quantize_mx(out=out_codes[:].bitcast(E4M3), scales=out_scales[4 * c : P, :], in_=woven[:])
+            nc.sync.dma_start(out=words[:, cols], in_=out_codes[:].bitcast(I32))
+        for quad in range(4):
+            queue = nc.scalar if quad % 2 else nc.sync
+            queue.dma_start(
+                out=out_2[0, 4 * quad : 4 * quad + 4, :].bitcast(I32).rearrange("i (c x) -> c i x", c=CHUNKS),
+                in_=out_scales[32 * quad : 32 * quad + 16, :].bitcast(I32),
+            )

@@ -21,7 +21,8 @@ PACK = 4
 CHUNK = 512
 CHUNKS = T // CHUNK
 DEAL_SPLIT = 64
-WEAVE_SPLIT = 352
+VECTOR_PAIRS = 1
+WEAVE_SPLIT = 88
 
 
 def tile_attend_gat_pl_tnh_k_kernel(tc, qT, kT, vT, doT, rw, qm, offs, out_0, out_1, out_2):
@@ -47,32 +48,42 @@ def tile_attend_gat_pl_tnh_k_kernel(tc, qT, kT, vT, doT, rw, qm, offs, out_0, ou
             nc.sync.dma_start(out=raw[:], in_=src[0].rearrange("(p j) w -> p j w", j=PACK))
             return raw
 
-        def mx_tiles(name, width):
-            codes = keep.tile([P, width], U32, name=name + "_codes", align_bytes=64)
-            scales = keep.tile([P, width], U8, name=name + "_scales", align_bytes=64)
+        def mx_tiles(name, width, codes_tag="", scales_tag=""):
+            codes = keep.tile([P, width], U32, name=name + "_codes", tag=codes_tag or name + "_codes", align_bytes=64)
+            scales = keep.tile([P, width], U8, name=name + "_scales", tag=scales_tag or name + "_scales", align_bytes=64)
             return codes, scales
+
+        def shared_copy(dst, src, split):
+            if split > 0:
+                nc.vector.tensor_copy(out=dst[:, :split], in_=src[:, :split])
+            if split < dst.shape[1]:
+                nc.scalar.copy(out=dst[:, split:], in_=src[:, split:])
+
+        def weave(rows, name, split):
+            woven = keep.tile([P, N * PACK], BF16, name=name, align_bytes=64)
+            dst = woven[:].rearrange("p (c i t) -> p c t i", i=4, t=PACK)
+            src = rows[:].rearrange("p t (c i) -> p c t i", i=4)
+            shared_copy(dst, src, split)
+            return woven
 
         def deal(raw, name, split):
             dealt = keep.tile([P, PACK * 512], BF16, name=name, align_bytes=64)
             dst = dealt[:].rearrange("p (t m j) -> p m j t", t=PACK, j=PACK)
             src = raw[:].rearrange("p j (m t) -> p m j t", t=PACK)
-            if split > 0:
-                nc.vector.tensor_copy(out=dst[:, :split], in_=src[:, :split])
-            nc.scalar.copy(out=dst[:, split:], in_=src[:, split:])
+            shared_copy(dst, src, split)
             return dealt
 
-        def quantize(src, codes, scales, fmt, first, count):
+        def quantize(src, codes, scales, fmt, first, count, base=0):
             nc.vector.quantize_mx(
-                out=codes[:, first : first + count].bitcast(fmt),
-                scales=scales[:, first : first + count],
+                out=codes[:, first - base : first - base + count].bitcast(fmt),
+                scales=scales[:, first - base : first - base + count],
                 in_=src[:, PACK * first : PACK * (first + count)],
             )
 
         def gather(planes, name):
-            picked = keep.tile([P, N * PACK], BF16, name=name, align_bytes=64)
-            lanes = picked[:].rearrange("p (n j) -> p n j", j=PACK)
+            picked = keep.tile([P, PACK, N], BF16, name=name, align_bytes=64)
             for j in range(PACK):
-                nc.vector.tensor_copy(out=lanes[:, :, j], in_=planes[j][:].indirect(offsets[:]))
+                nc.vector.tensor_copy(out=picked[:, j, :], in_=planes[j][:].indirect(offsets[:]))
             return picked
 
         def product(bank, stat, stat_fmt, t, mov, mov_fmt):
@@ -99,24 +110,27 @@ def tile_attend_gat_pl_tnh_k_kernel(tc, qT, kT, vT, doT, rw, qm, offs, out_0, ou
         windows = []
         for j in range(PACK):
             window = keep.tile([P, T], F32, name="window" + str(j), align_bytes=64)
-            nc.gpsimd.memset(window[:], 0.0)
+            engine = nc.vector if j < 2 else nc.gpsimd
+            engine.memset(window[:].bitcast(I32), 0)
             windows.append(window)
 
         k_mx = mx_tiles("k", N)
-        quantize(gather(k_planes, "k_picked"), *k_mx, E4M3, 0, N)
+        quantize(weave(gather(k_planes, "k_picked"), "k_woven", WEAVE_SPLIT), *k_mx, E4M3, 0, N)
         q_mx = mx_tiles("q", R)
-        quantize(deal(q_raw, "q_dealt", DEAL_SPLIT), *q_mx, E4M3, 0, R)
+        q_dealt = deal(q_raw, "q_dealt", DEAL_SPLIT)
+        for t in range(PACK):
+            quantize(q_dealt, *q_mx, E4M3, t * P, P)
         neg_gate = keep.tile([P, PACK], F32, name="neg_gate")
         nc.vector.tensor_scalar(out=neg_gate[:], in0=gate[:], scalar1=-1.0, scalar2=None, op0=ALU.mult)
         slopes = []
         for t in range(PACK):
             bank = psum.tile([P, N], F32, name="score" + str(t), tag="bank" + str(t))
             product(bank, q_mx, E4M3, t, k_mx, E4M3)
-            weight = keep.tile([P, N], F32, name="weight" + str(t), tag="weight", bufs=2)
+            weight = keep.tile([P, N], F32, name="weight" + str(t))
             nc.scalar.activation(out=weight[:], in_=bank[:], func=ACT.Tanh)
-            square = keep.tile([P, N], F32, name="square" + str(t), tag="square", bufs=2)
+            square = keep.tile([P, N], F32, name="square" + str(t))
             nc.scalar.activation(out=square[:], in_=weight[:], func=ACT.Square)
-            slope = keep.tile([P, N], F32, name="slope" + str(t))
+            slope = keep.tile([P, N], F32, name="slope" + str(t), align_bytes=64)
             nc.vector.tensor_scalar(
                 out=slope[:], in0=square[:], scalar1=neg_gate[:, t : t + 1], scalar2=gate[:, t : t + 1],
                 op0=ALU.mult, op1=ALU.add,
@@ -124,7 +138,7 @@ def tile_attend_gat_pl_tnh_k_kernel(tc, qT, kT, vT, doT, rw, qm, offs, out_0, ou
             slopes.append(slope)
 
         v_mx = mx_tiles("v", N)
-        quantize(gather(v_planes, "v_picked"), *v_mx, E4M3, 0, N)
+        quantize(weave(gather(v_planes, "v_picked"), "v_woven", WEAVE_SPLIT), *v_mx, E4M3, 0, N)
         do_mx = mx_tiles("do", R)
         do_dealt = deal(do_raw, "do_dealt", DEAL_SPLIT)
         for t in range(PACK):
@@ -134,18 +148,15 @@ def tile_attend_gat_pl_tnh_k_kernel(tc, qT, kT, vT, doT, rw, qm, offs, out_0, ou
             bank = psum.tile([P, N], F32, name="dp" + str(t), tag="bank" + str(PACK + t))
             product(bank, do_mx, E5M2, t, v_mx, E4M3)
             nc.vector.tensor_tensor(out=ds_rows[:, t, :], in0=bank[:], in1=slopes[t][:], op=ALU.mult)
-        ds_woven = keep.tile([P, N * PACK], BF16, name="ds_woven", align_bytes=64)
-        dst = ds_woven[:].rearrange("p (c i t) -> p c t i", i=4, t=PACK)
-        src = ds_rows[:].rearrange("p t (c i) -> p c t i", i=4)
-        nc.vector.tensor_copy(out=dst[:, : WEAVE_SPLIT // 4], in_=src[:, : WEAVE_SPLIT // 4])
-        nc.scalar.copy(out=dst[:, WEAVE_SPLIT // 4 :], in_=src[:, WEAVE_SPLIT // 4 :])
-        ds_mx = mx_tiles("ds", N)
-        quantize(ds_woven, *ds_mx, E5M2, 0, N)
-
-        qm_mx = mx_tiles("qm", D)
+        ds_woven = weave(ds_rows, "ds_woven", WEAVE_SPLIT)
         qm_dealt = deal(qm_raw, "qm_dealt", 0)
-        for j in range(PACK):
-            quantize(qm_dealt, *qm_mx, E4M3, j * P, P)
+        qm_first = mx_tiles("qm_first", P, "slope3")
+        quantize(qm_dealt, *qm_first, E4M3, 0, P)
+        ds_mx = mx_tiles("ds", N, "hold0", "hold1")
+        quantize(ds_woven, *ds_mx, E5M2, 0, N)
+        qm_rest = mx_tiles("qm_rest", D - P, "ds_woven", "hold3")
+        for j in range(1, PACK):
+            quantize(qm_dealt, *qm_rest, E4M3, j * P, P, P)
         grads = []
 
         def pieces(j):
@@ -153,13 +164,17 @@ def tile_attend_gat_pl_tnh_k_kernel(tc, qT, kT, vT, doT, rw, qm, offs, out_0, ou
 
         for j in range(PACK):
             bank = psum.tile([P, N], F32, name="dk" + str(j), tag="bank" + str(j))
-            product(bank, qm_mx, E4M3, j, ds_mx, E5M2)
+            if j == 0:
+                product(bank, qm_first, E4M3, 0, ds_mx, E5M2)
+            else:
+                product(bank, qm_rest, E4M3, j - 1, ds_mx, E5M2)
             grad = keep.tile([P, N], F32, name="grad" + str(j))
             for lo, hi in pieces(j):
                 nc.scalar.copy(out=grad[:, lo:hi], in_=bank[:, lo:hi])
             grads.append(grad)
 
-        pairs = [big.tile([P, 2, CHUNK, 2], BF16, name="pairs" + str(c), tag="kpool", align_bytes=64) for c in range(CHUNKS)]
+        holds = ("hold0", "hold1", "ds_woven", "hold3")
+        pairs = [keep.tile([P, 2, CHUNK, 2], BF16, name="pairs" + str(c), tag=holds[c], align_bytes=64) for c in range(CHUNKS)]
         out_rows = out_0.rearrange("(p j) t -> p j t", j=PACK)
         for j in range(PACK):
             for lo, hi in pieces(j):
@@ -168,17 +183,18 @@ def tile_attend_gat_pl_tnh_k_kernel(tc, qT, kT, vT, doT, rw, qm, offs, out_0, ou
             for c in range(CHUNKS):
                 dst = pairs[c][:, j // 2, :, j % 2]
                 src = windows[j][:, c * CHUNK : (c + 1) * CHUNK]
-                if j == PACK - 1 and c == 0:
+                if j == PACK - 1 and c < VECTOR_PAIRS:
                     nc.vector.tensor_copy(out=dst, in_=src)
-                elif j == PACK - 2 and c == 0:
+                elif j == PACK - 2 and c < VECTOR_PAIRS:
                     nc.scalar.copy(out=pairs[c][:, j // 2], in_=src.unsqueeze(2).to_broadcast([P, CHUNK, 2]))
                 else:
                     nc.scalar.copy(out=dst, in_=src)
 
         out_scales = keep.tile([P, CHUNK], U8, name="out_scales", align_bytes=64)
         words = out_1[0].rearrange("p t l -> p (t l)").bitcast(I32)
-        for c in range(CHUNKS):
-            cols = slice(c * CHUNK, (c + 1) * CHUNK)
+        wovens = {}
+
+        def join(c):
             woven = big.tile([P, CHUNK * PACK], BF16, name="woven" + str(c), tag="vpool", align_bytes=64)
             dst = woven[:].bitcast(F32).rearrange("p (g i u) -> p g u i", i=4, u=2)
             src = pairs[c][:].rearrange("p u n e -> p u (n e)").bitcast(F32).rearrange("p u (g i) -> p g u i", i=4)
@@ -186,9 +202,18 @@ def tile_attend_gat_pl_tnh_k_kernel(tc, qT, kT, vT, doT, rw, qm, offs, out_0, ou
                 nc.scalar.copy(out=dst, in_=src)
             else:
                 nc.vector.tensor_copy(out=dst, in_=src)
-            out_codes = keep.tile([P, CHUNK], U32, name="out_codes" + str(c), align_bytes=64)
-            nc.vector.quantize_mx(out=out_codes[:].bitcast(E4M3), scales=out_scales[4 * c : P, :], in_=woven[:])
-            nc.sync.dma_start(out=words[:, cols], in_=out_codes[:].bitcast(I32))
+            wovens[c] = woven
+
+        def emit(c):
+            out_codes = keep.tile([P, CHUNK], U32, name="out_codes" + str(c), tag=holds[c + 1] if c < 2 else "out_codes" + str(c), align_bytes=64)
+            nc.vector.quantize_mx(out=out_codes[:].bitcast(E4M3), scales=out_scales[4 * c : P, :], in_=wovens[c][:])
+            nc.sync.dma_start(out=words[:, c * CHUNK : (c + 1) * CHUNK], in_=out_codes[:].bitcast(I32))
+
+        join(0)
+        for c in range(CHUNKS):
+            if c + 1 < CHUNKS:
+                join(c + 1)
+            emit(c)
         for quad in range(4):
             queue = nc.scalar if quad % 2 else nc.sync
             queue.dma_start(

@@ -20,8 +20,12 @@ P = 128
 PACK = 4
 CHUNK = 512
 CHUNKS = T // CHUNK
-DEAL_SPLIT = 64
-VECTOR_PAIRS = 1
+DEAL_SPLIT = 30
+PIECES = (512, 512, 256, 256, 256, 256)
+SCALAR_JOINS = 3
+VECTOR_PAIRS = 2
+DO_SPLIT = 36
+STORE_ENDS = (1024, 1536, 1792, 2048)
 WEAVE_SPLIT = 88
 
 
@@ -68,8 +72,8 @@ def tile_attend_gat_pl_tnh_k_kernel(tc, qT, kT, vT, doT, rw, qm, offs, out_0, ou
 
         def deal(raw, name, split):
             dealt = keep.tile([P, PACK * 512], BF16, name=name, align_bytes=64)
-            dst = dealt[:].rearrange("p (t m j) -> p m j t", t=PACK, j=PACK)
-            src = raw[:].rearrange("p j (m t) -> p m j t", t=PACK)
+            dst = dealt[:].rearrange("p (t m h j) -> p m j h t", t=PACK, h=2, j=PACK)
+            src = raw[:].rearrange("p j (m h t) -> p m j h t", h=2, t=PACK)
             shared_copy(dst, src, split)
             return dealt
 
@@ -84,6 +88,13 @@ def tile_attend_gat_pl_tnh_k_kernel(tc, qT, kT, vT, doT, rw, qm, offs, out_0, ou
             picked = keep.tile([P, PACK, N], BF16, name=name, align_bytes=64)
             for j in range(PACK):
                 nc.vector.tensor_copy(out=picked[:, j, :], in_=planes[j][:].indirect(offsets[:]))
+            return picked
+
+        def gather_woven(planes, name):
+            picked = keep.tile([P, N * PACK], BF16, name=name, align_bytes=64)
+            lanes = picked[:].rearrange("p (n j) -> p n j", j=PACK)
+            for j in range(PACK):
+                nc.vector.tensor_copy(out=lanes[:, :, j], in_=planes[j][:].indirect(offsets[:]))
             return picked
 
         def product(bank, stat, stat_fmt, t, mov, mov_fmt):
@@ -138,9 +149,9 @@ def tile_attend_gat_pl_tnh_k_kernel(tc, qT, kT, vT, doT, rw, qm, offs, out_0, ou
             slopes.append(slope)
 
         v_mx = mx_tiles("v", N)
-        quantize(weave(gather(v_planes, "v_picked"), "v_woven", WEAVE_SPLIT), *v_mx, E4M3, 0, N)
+        quantize(gather_woven(v_planes, "v_woven"), *v_mx, E4M3, 0, N)
         do_mx = mx_tiles("do", R)
-        do_dealt = deal(do_raw, "do_dealt", DEAL_SPLIT)
+        do_dealt = deal(do_raw, "do_dealt", DO_SPLIT)
         for t in range(PACK):
             quantize(do_dealt, *do_mx, E5M2, t * P, P)
         ds_rows = keep.tile([P, PACK, N], BF16, name="ds_rows", align_bytes=64)
@@ -152,9 +163,9 @@ def tile_attend_gat_pl_tnh_k_kernel(tc, qT, kT, vT, doT, rw, qm, offs, out_0, ou
         qm_dealt = deal(qm_raw, "qm_dealt", 0)
         qm_first = mx_tiles("qm_first", P, "slope3")
         quantize(qm_dealt, *qm_first, E4M3, 0, P)
-        ds_mx = mx_tiles("ds", N, "hold0", "hold1")
+        ds_mx = mx_tiles("ds", N, "pairs")
         quantize(ds_woven, *ds_mx, E5M2, 0, N)
-        qm_rest = mx_tiles("qm_rest", D - P, "ds_woven", "hold3")
+        qm_rest = mx_tiles("qm_rest", D - P, "ds_woven")
         for j in range(1, PACK):
             quantize(qm_dealt, *qm_rest, E4M3, j * P, P, P)
         grads = []
@@ -173,45 +184,55 @@ def tile_attend_gat_pl_tnh_k_kernel(tc, qT, kT, vT, doT, rw, qm, offs, out_0, ou
                 nc.scalar.copy(out=grad[:, lo:hi], in_=bank[:, lo:hi])
             grads.append(grad)
 
-        holds = ("hold0", "hold1", "ds_woven", "hold3")
-        pairs = [keep.tile([P, 2, CHUNK, 2], BF16, name="pairs" + str(c), tag=holds[c], align_bytes=64) for c in range(CHUNKS)]
+        pairs = keep.tile([P, 2 * T * 2], BF16, name="pairs", tag="pairs", align_bytes=64)
+        halves = pairs[:].rearrange("p (u n e) -> p u n e", u=2, e=2)
+        pair_words = pairs[:].bitcast(F32).rearrange("p (u n) -> p u n", u=2)
+        starts = [sum(PIECES[:c]) for c in range(len(PIECES))]
         out_rows = out_0.rearrange("(p j) t -> p j t", j=PACK)
         for j in range(PACK):
             for lo, hi in pieces(j):
                 nc.vector.tensor_copy(out=windows[j][:].indirect(offsets[:, lo // 16 : hi // 16]), in_=grads[j][:, lo:hi])
             nc.sync.dma_start(out=out_rows[:, j, :], in_=windows[j][:])
-            for c in range(CHUNKS):
-                dst = pairs[c][:, j // 2, :, j % 2]
-                src = windows[j][:, c * CHUNK : (c + 1) * CHUNK]
-                if j == PACK - 1 and c < VECTOR_PAIRS:
-                    nc.vector.tensor_copy(out=dst, in_=src)
-                elif j == PACK - 2 and c < VECTOR_PAIRS:
-                    nc.scalar.copy(out=pairs[c][:, j // 2], in_=src.unsqueeze(2).to_broadcast([P, CHUNK, 2]))
-                else:
-                    nc.scalar.copy(out=dst, in_=src)
+            if j < PACK - 2:
+                nc.scalar.copy(out=halves[:, j // 2, :, j % 2], in_=windows[j][:])
+            elif j == PACK - 2:
+                cut = starts[VECTOR_PAIRS]
+                nc.scalar.copy(out=halves[:, 1, :cut, :], in_=windows[j][:, :cut].unsqueeze(2).to_broadcast([P, cut, 2]))
+                nc.scalar.copy(out=halves[:, 1, cut:, 0], in_=windows[j][:, cut:])
+            else:
+                for c, (lo, width) in enumerate(zip(starts, PIECES)):
+                    engine_copy = nc.vector.tensor_copy if c < VECTOR_PAIRS else nc.scalar.copy
+                    engine_copy(out=halves[:, 1, lo : lo + width, 1], in_=windows[j][:, lo : lo + width])
 
         out_scales = keep.tile([P, CHUNK], U8, name="out_scales", align_bytes=64)
         words = out_1[0].rearrange("p t l -> p (t l)").bitcast(I32)
+        out_codes = keep.tile([P, T], U32, name="out_codes", align_bytes=64)
         wovens = {}
 
         def join(c):
-            woven = big.tile([P, CHUNK * PACK], BF16, name="woven" + str(c), tag="vpool", align_bytes=64)
+            lo, width = starts[c], PIECES[c]
+            woven = big.tile([P, width * PACK], BF16, name="woven" + str(c), tag="kpool" if c < 4 else "vpool", align_bytes=64)
             dst = woven[:].bitcast(F32).rearrange("p (g i u) -> p g u i", i=4, u=2)
-            src = pairs[c][:].rearrange("p u n e -> p u (n e)").bitcast(F32).rearrange("p u (g i) -> p g u i", i=4)
-            if c == CHUNKS - 1:
+            src = pair_words[:, :, lo : lo + width].rearrange("p u (g i) -> p g u i", i=4)
+            if c >= len(PIECES) - SCALAR_JOINS:
                 nc.scalar.copy(out=dst, in_=src)
             else:
                 nc.vector.tensor_copy(out=dst, in_=src)
             wovens[c] = woven
 
         def emit(c):
-            out_codes = keep.tile([P, CHUNK], U32, name="out_codes" + str(c), tag=holds[c + 1] if c < 2 else "out_codes" + str(c), align_bytes=64)
-            nc.vector.quantize_mx(out=out_codes[:].bitcast(E4M3), scales=out_scales[4 * c : P, :], in_=wovens[c][:])
-            nc.sync.dma_start(out=words[:, c * CHUNK : (c + 1) * CHUNK], in_=out_codes[:].bitcast(I32))
+            lo, width = starts[c], PIECES[c]
+            row, col = 4 * (lo // CHUNK), lo % CHUNK
+            nc.vector.quantize_mx(
+                out=out_codes[:, lo : lo + width].bitcast(E4M3), scales=out_scales[row:P, col : col + width], in_=wovens[c][:]
+            )
+            if lo + width in STORE_ENDS:
+                first = max([0] + [end for end in STORE_ENDS if end <= lo])
+                nc.sync.dma_start(out=words[:, first : lo + width], in_=out_codes[:, first : lo + width].bitcast(I32))
 
         join(0)
-        for c in range(CHUNKS):
-            if c + 1 < CHUNKS:
+        for c in range(len(PIECES)):
+            if c + 1 < len(PIECES):
                 join(c + 1)
             emit(c)
         for quad in range(4):

@@ -17,88 +17,69 @@ ACT = mybir.ActivationFunctionType
 ALU = mybir.AluOpType
 
 P = 128
-PACK = 4
-CHUNK = 512
-CHUNKS = T // CHUNK
-DEAL_SPLIT = 30
-PIECES = (512, 512, 256, 256, 256, 256)
-SCALAR_JOINS = 3
-VECTOR_PAIRS = 2
-DO_SPLIT = 36
-STORE_ENDS = (1024, 1536, 1792, 2048)
+LANES = 4
+RUN = 4
+
 WEAVE_SPLIT = 88
+Q_DEAL_SPLIT = 30
+DO_DEAL_SPLIT = 36
+
+PIECES = (512, 512, 256, 256, 256, 256)
+VECTOR_ROUNDS = 2
+VECTOR_JOINS = 3
+STEP = 256
+SPAN = 512
+STORE_ENDS = (512, 1280, 1792, 2048)
 
 
 def tile_attend_gat_pl_tnh_k_kernel(tc, qT, kT, vT, doT, rw, qm, offs, out_0, out_1, out_2):
     nc = tc.nc
     with ExitStack() as ctx:
         keep = ctx.enter_context(tc.tile_pool(name="keep", bufs=1))
-        big = ctx.enter_context(tc.tile_pool(name="big", bufs=4))
+        big = ctx.enter_context(tc.tile_pool(name="big", bufs=LANES))
         psum = ctx.enter_context(tc.psum_pool(name="psum", bufs=1))
 
-        def load_pool(src, tag, offsets=None):
-            planes = []
-            rows = src.rearrange("(p j) t -> p j t", j=PACK)
-            for j in range(PACK):
-                plane = big.tile([P, T], F32, name=tag + str(j), tag=tag, align_bytes=64)
-                nc.sync.dma_start(out=plane[:], in_=rows[:, j, :])
-                planes.append(plane)
-                if j == 0 and offsets is not None:
-                    nc.sync.dma_start(offsets[:], offs)
-            return planes
+        def load_plane(src, j, tag):
+            plane = big.tile([P, T], F32, name=tag + str(j), tag=tag, align_bytes=64)
+            nc.sync.dma_start(out=plane[:], in_=src.rearrange("(p j) t -> p j t", j=LANES)[:, j, :])
+            return plane
 
         def load_square(src, name):
-            raw = keep.tile([P, PACK, 512], F32, name=name, align_bytes=64)
-            nc.sync.dma_start(out=raw[:], in_=src[0].rearrange("(p j) w -> p j w", j=PACK))
+            raw = keep.tile([P, LANES, 512], F32, name=name, align_bytes=64)
+            nc.sync.dma_start(out=raw[:], in_=src[0].rearrange("(p j) w -> p j w", j=LANES))
             return raw
 
-        def mx_tiles(name, width, codes_tag="", scales_tag=""):
+        def mx_tiles(name, width, codes_tag=""):
             codes = keep.tile([P, width], U32, name=name + "_codes", tag=codes_tag or name + "_codes", align_bytes=64)
-            scales = keep.tile([P, width], U8, name=name + "_scales", tag=scales_tag or name + "_scales", align_bytes=64)
+            scales = keep.tile([P, width], U8, name=name + "_scales", tag=name + "_scales", align_bytes=64)
             return codes, scales
 
         def shared_copy(dst, src, split):
-            if split > 0:
-                nc.vector.tensor_copy(out=dst[:, :split], in_=src[:, :split])
-            if split < dst.shape[1]:
-                nc.scalar.copy(out=dst[:, split:], in_=src[:, split:])
+            nc.vector.tensor_copy(out=dst[:, :split], in_=src[:, :split])
+            nc.scalar.copy(out=dst[:, split:], in_=src[:, split:])
 
-        def weave(rows, name, split):
-            woven = keep.tile([P, N * PACK], BF16, name=name, align_bytes=64)
-            dst = woven[:].rearrange("p (c i t) -> p c t i", i=4, t=PACK)
-            src = rows[:].rearrange("p t (c i) -> p c t i", i=4)
-            shared_copy(dst, src, split)
+        def weave(planes, name):
+            woven = keep.tile([P, N * LANES], BF16, name=name, align_bytes=64)
+            dst = woven[:].rearrange("p (c i t) -> p c t i", i=RUN, t=LANES)
+            src = planes[:].rearrange("p t (c i) -> p c t i", i=RUN)
+            shared_copy(dst, src, WEAVE_SPLIT)
             return woven
 
-        def deal(raw, name, split):
-            dealt = keep.tile([P, PACK * 512], BF16, name=name, align_bytes=64)
-            dst = dealt[:].rearrange("p (t m h j) -> p m j h t", t=PACK, h=2, j=PACK)
-            src = raw[:].rearrange("p j (m h t) -> p m j h t", h=2, t=PACK)
-            shared_copy(dst, src, split)
-            return dealt
+        def deal_views(raw, name):
+            dealt = keep.tile([P, LANES * 512], BF16, name=name, align_bytes=64)
+            dst = dealt[:].rearrange("p (t g h j) -> p g j h t", t=LANES, h=2, j=LANES)
+            src = raw[:].rearrange("p j (g h t) -> p g j h t", h=2, t=LANES)
+            return dealt, dst, src
 
-        def quantize(src, codes, scales, fmt, first, count, base=0):
+        def quantize(src, first, count, mx, fmt, at):
             nc.vector.quantize_mx(
-                out=codes[:, first - base : first - base + count].bitcast(fmt),
-                scales=scales[:, first - base : first - base + count],
-                in_=src[:, PACK * first : PACK * (first + count)],
+                out=mx[0][:, at : at + count].bitcast(fmt),
+                scales=mx[1][:, at : at + count],
+                in_=src[:, LANES * first : LANES * (first + count)],
             )
 
-        def gather(planes, name):
-            picked = keep.tile([P, PACK, N], BF16, name=name, align_bytes=64)
-            for j in range(PACK):
-                nc.vector.tensor_copy(out=picked[:, j, :], in_=planes[j][:].indirect(offsets[:]))
-            return picked
-
-        def gather_woven(planes, name):
-            picked = keep.tile([P, N * PACK], BF16, name=name, align_bytes=64)
-            lanes = picked[:].rearrange("p (n j) -> p n j", j=PACK)
-            for j in range(PACK):
-                nc.vector.tensor_copy(out=lanes[:, :, j], in_=planes[j][:].indirect(offsets[:]))
-            return picked
-
-        def product(bank, stat, stat_fmt, t, mov, mov_fmt):
-            cols = slice(t * P, (t + 1) * P)
+        def product(bank, stat, stat_fmt, tile, mov, mov_fmt):
+            cols = slice(tile * P, (tile + 1) * P)
             nc.tensor.matmul_mx(
                 out=bank[:],
                 lhsT=stat[0][:, cols].bitcast(stat_fmt),
@@ -110,31 +91,35 @@ def tile_attend_gat_pl_tnh_k_kernel(tc, qT, kT, vT, doT, rw, qm, offs, out_0, ou
             )
 
         offsets = keep.tile([P, N // 16], U16, name="offsets")
-        k_planes = load_pool(kT, "kpool", offsets)
+        k_planes = [load_plane(kT, 0, "kpool")]
+        nc.sync.dma_start(offsets[:], offs)
+        k_planes.extend(load_plane(kT, j, "kpool") for j in range(1, LANES))
         q_raw = load_square(qT, "q_raw")
-        gate = keep.tile([P, PACK], F32, name="gate")
-        nc.sync.dma_start(out=gate[:], in_=rw[0].rearrange("(p j) o -> p (j o)", j=PACK))
-        v_planes = load_pool(vT, "vpool")
+        v_planes = [load_plane(vT, j, "vpool") for j in range(LANES)]
         do_raw = load_square(doT, "do_raw")
+        gate = keep.tile([P, LANES], F32, name="gate")
+        nc.sync.dma_start(out=gate[:], in_=rw[0].rearrange("(p j) o -> p (j o)", j=LANES))
         qm_raw = load_square(qm, "qm_raw")
 
         windows = []
-        for j in range(PACK):
+        for j in range(LANES):
             window = keep.tile([P, T], F32, name="window" + str(j), align_bytes=64)
-            engine = nc.vector if j < 2 else nc.gpsimd
+            engine = nc.vector if j < LANES // 2 else nc.gpsimd
             engine.memset(window[:].bitcast(I32), 0)
             windows.append(window)
 
+        k_picked = keep.tile([P, LANES, N], BF16, name="k_picked", align_bytes=64)
+        for j in range(LANES):
+            nc.vector.tensor_copy(out=k_picked[:, j, :], in_=k_planes[j][:].indirect(offsets[:]))
         k_mx = mx_tiles("k", N)
-        quantize(weave(gather(k_planes, "k_picked"), "k_woven", WEAVE_SPLIT), *k_mx, E4M3, 0, N)
+        quantize(weave(k_picked, "k_woven"), 0, N, k_mx, E4M3, 0)
         q_mx = mx_tiles("q", R)
-        q_dealt = deal(q_raw, "q_dealt", DEAL_SPLIT)
-        for t in range(PACK):
-            quantize(q_dealt, *q_mx, E4M3, t * P, P)
-        neg_gate = keep.tile([P, PACK], F32, name="neg_gate")
-        nc.vector.tensor_scalar(out=neg_gate[:], in0=gate[:], scalar1=-1.0, scalar2=None, op0=ALU.mult)
+        q_dealt, dst, src = deal_views(q_raw, "q_dealt")
+        shared_copy(dst, src, Q_DEAL_SPLIT)
+        for t in range(LANES):
+            quantize(q_dealt, t * P, P, q_mx, E4M3, t * P)
         slopes = []
-        for t in range(PACK):
+        for t in range(LANES):
             bank = psum.tile([P, N], F32, name="score" + str(t), tag="bank" + str(t))
             product(bank, q_mx, E4M3, t, k_mx, E4M3)
             weight = keep.tile([P, N], F32, name="weight" + str(t))
@@ -142,93 +127,94 @@ def tile_attend_gat_pl_tnh_k_kernel(tc, qT, kT, vT, doT, rw, qm, offs, out_0, ou
             square = keep.tile([P, N], F32, name="square" + str(t))
             nc.scalar.activation(out=square[:], in_=weight[:], func=ACT.Square)
             slope = keep.tile([P, N], F32, name="slope" + str(t), align_bytes=64)
-            nc.vector.tensor_scalar(
-                out=slope[:], in0=square[:], scalar1=neg_gate[:, t : t + 1], scalar2=gate[:, t : t + 1],
-                op0=ALU.mult, op1=ALU.add,
-            )
+            nc.vector.tensor_scalar(out=slope[:], in0=square[:], scalar1=-1.0, scalar2=1.0, op0=ALU.mult, op1=ALU.add)
             slopes.append(slope)
 
+        v_woven = keep.tile([P, N * LANES], BF16, name="v_woven", align_bytes=64)
+        v_lanes = v_woven[:].rearrange("p (n j) -> p n j", j=LANES)
+        for j in range(LANES):
+            nc.vector.tensor_copy(out=v_lanes[:, :, j], in_=v_planes[j][:].indirect(offsets[:]))
         v_mx = mx_tiles("v", N)
-        quantize(gather_woven(v_planes, "v_woven"), *v_mx, E4M3, 0, N)
+        quantize(v_woven, 0, N, v_mx, E4M3, 0)
         do_mx = mx_tiles("do", R)
-        do_dealt = deal(do_raw, "do_dealt", DO_SPLIT)
-        for t in range(PACK):
-            quantize(do_dealt, *do_mx, E5M2, t * P, P)
-        ds_rows = keep.tile([P, PACK, N], BF16, name="ds_rows", align_bytes=64)
-        for t in range(PACK):
-            bank = psum.tile([P, N], F32, name="dp" + str(t), tag="bank" + str(PACK + t))
+        do_dealt, dst, src = deal_views(do_raw, "do_dealt")
+        shared_copy(dst, src, DO_DEAL_SPLIT)
+        for t in range(LANES):
+            quantize(do_dealt, t * P, P, do_mx, E5M2, t * P)
+        ds_planes = keep.tile([P, LANES, N], BF16, name="ds_planes", align_bytes=64)
+        for t in range(LANES):
+            bank = psum.tile([P, N], F32, name="dp" + str(t), tag="bank" + str(LANES + t))
             product(bank, do_mx, E5M2, t, v_mx, E4M3)
-            nc.vector.tensor_tensor(out=ds_rows[:, t, :], in0=bank[:], in1=slopes[t][:], op=ALU.mult)
-        ds_woven = weave(ds_rows, "ds_woven", WEAVE_SPLIT)
-        qm_dealt = deal(qm_raw, "qm_dealt", 0)
-        qm_first = mx_tiles("qm_first", P, "slope3")
-        quantize(qm_dealt, *qm_first, E4M3, 0, P)
+            nc.vector.scalar_tensor_tensor(
+                out=ds_planes[:, t, :], in0=bank[:], scalar=gate[:, t : t + 1], in1=slopes[t][:], op0=ALU.mult, op1=ALU.mult
+            )
+        ds_woven = weave(ds_planes, "ds_woven")
+
+        qm_dealt, dst, src = deal_views(qm_raw, "qm_dealt")
+        nc.scalar.copy(out=dst, in_=src)
+        qm_first = mx_tiles("qm_first", P, "slope" + str(LANES - 1))
+        quantize(qm_dealt, 0, P, qm_first, E4M3, 0)
         ds_mx = mx_tiles("ds", N, "pairs")
-        quantize(ds_woven, *ds_mx, E5M2, 0, N)
+        quantize(ds_woven, 0, N, ds_mx, E5M2, 0)
         qm_rest = mx_tiles("qm_rest", D - P, "ds_woven")
-        for j in range(1, PACK):
-            quantize(qm_dealt, *qm_rest, E4M3, j * P, P, P)
+        for j in range(1, LANES):
+            quantize(qm_dealt, j * P, P, qm_rest, E4M3, (j - 1) * P)
         grads = []
-
-        def pieces(j):
-            return ((0, N // 2), (N // 2, N)) if j == 0 else ((0, N),)
-
-        for j in range(PACK):
+        for j in range(LANES):
             bank = psum.tile([P, N], F32, name="dk" + str(j), tag="bank" + str(j))
             if j == 0:
                 product(bank, qm_first, E4M3, 0, ds_mx, E5M2)
             else:
                 product(bank, qm_rest, E4M3, j - 1, ds_mx, E5M2)
             grad = keep.tile([P, N], F32, name="grad" + str(j))
-            for lo, hi in pieces(j):
-                nc.scalar.copy(out=grad[:, lo:hi], in_=bank[:, lo:hi])
+            nc.scalar.copy(out=grad[:], in_=bank[:])
             grads.append(grad)
 
         pairs = keep.tile([P, 2 * T * 2], BF16, name="pairs", tag="pairs", align_bytes=64)
         halves = pairs[:].rearrange("p (u n e) -> p u n e", u=2, e=2)
         pair_words = pairs[:].bitcast(F32).rearrange("p (u n) -> p u n", u=2)
         starts = [sum(PIECES[:c]) for c in range(len(PIECES))]
-        out_rows = out_0.rearrange("(p j) t -> p j t", j=PACK)
-        for j in range(PACK):
-            for lo, hi in pieces(j):
-                nc.vector.tensor_copy(out=windows[j][:].indirect(offsets[:, lo // 16 : hi // 16]), in_=grads[j][:, lo:hi])
-            nc.sync.dma_start(out=out_rows[:, j, :], in_=windows[j][:])
-            if j < PACK - 2:
-                nc.scalar.copy(out=halves[:, j // 2, :, j % 2], in_=windows[j][:])
-            elif j == PACK - 2:
-                cut = starts[VECTOR_PAIRS]
+        cut = starts[VECTOR_ROUNDS]
+        out_planes = out_0.rearrange("(p j) t -> p j t", j=LANES)
+        for j in range(LANES):
+            nc.vector.tensor_copy(out=windows[j][:].indirect(offsets[:]), in_=grads[j][:])
+            nc.sync.dma_start(out=out_planes[:, j, :], in_=windows[j][:])
+            if j < 2:
+                nc.scalar.copy(out=halves[:, 0, :, j], in_=windows[j][:])
+            elif j == 2:
                 nc.scalar.copy(out=halves[:, 1, :cut, :], in_=windows[j][:, :cut].unsqueeze(2).to_broadcast([P, cut, 2]))
                 nc.scalar.copy(out=halves[:, 1, cut:, 0], in_=windows[j][:, cut:])
             else:
                 for c, (lo, width) in enumerate(zip(starts, PIECES)):
-                    engine_copy = nc.vector.tensor_copy if c < VECTOR_PAIRS else nc.scalar.copy
+                    engine_copy = nc.vector.tensor_copy if c < VECTOR_ROUNDS else nc.scalar.copy
                     engine_copy(out=halves[:, 1, lo : lo + width, 1], in_=windows[j][:, lo : lo + width])
 
-        out_scales = keep.tile([P, CHUNK], U8, name="out_scales", align_bytes=64)
-        words = out_1[0].rearrange("p t l -> p (t l)").bitcast(I32)
+        out_scales = keep.tile([P, SPAN], U8, name="out_scales", align_bytes=64)
+        out_words = out_1[0].rearrange("p t l -> p (t l)").bitcast(I32)
         out_codes = keep.tile([P, T], U32, name="out_codes", align_bytes=64)
-        wovens = {}
+        joined = {}
 
         def join(c):
             lo, width = starts[c], PIECES[c]
-            woven = big.tile([P, width * PACK], BF16, name="woven" + str(c), tag="kpool" if c < 4 else "vpool", align_bytes=64)
-            dst = woven[:].bitcast(F32).rearrange("p (g i u) -> p g u i", i=4, u=2)
-            src = pair_words[:, :, lo : lo + width].rearrange("p u (g i) -> p g u i", i=4)
-            if c >= len(PIECES) - SCALAR_JOINS:
-                nc.scalar.copy(out=dst, in_=src)
-            else:
-                nc.vector.tensor_copy(out=dst, in_=src)
-            wovens[c] = woven
+            tag = "kpool" if c < LANES else "vpool"
+            woven = big.tile([P, width * LANES], BF16, name="woven" + str(c), tag=tag, align_bytes=64)
+            dst = woven[:].bitcast(F32).rearrange("p (g i u) -> p g u i", i=RUN, u=2)
+            src = pair_words[:, :, lo : lo + width].rearrange("p u (g i) -> p g u i", i=RUN)
+            engine_copy = nc.vector.tensor_copy if c < VECTOR_JOINS else nc.scalar.copy
+            engine_copy(out=dst, in_=src)
+            joined[c] = woven
 
         def emit(c):
-            lo, width = starts[c], PIECES[c]
-            row, col = 4 * (lo // CHUNK), lo % CHUNK
-            nc.vector.quantize_mx(
-                out=out_codes[:, lo : lo + width].bitcast(E4M3), scales=out_scales[row:P, col : col + width], in_=wovens[c][:]
-            )
-            if lo + width in STORE_ENDS:
-                first = max([0] + [end for end in STORE_ENDS if end <= lo])
-                nc.sync.dma_start(out=words[:, first : lo + width], in_=out_codes[:, first : lo + width].bitcast(I32))
+            for lo in range(starts[c], starts[c] + PIECES[c], STEP):
+                row, col = 4 * (lo // SPAN), lo % SPAN
+                nc.vector.quantize_mx(
+                    out=out_codes[:, lo : lo + STEP].bitcast(E4M3),
+                    scales=out_scales[row:P, col : col + STEP],
+                    in_=joined[c][:, LANES * (lo - starts[c]) : LANES * (lo - starts[c] + STEP)],
+                )
+                if lo + STEP in STORE_ENDS:
+                    first = max([0] + [end for end in STORE_ENDS if end <= lo])
+                    nc.sync.dma_start(out=out_words[:, first : lo + STEP], in_=out_codes[:, first : lo + STEP].bitcast(I32))
 
         join(0)
         for c in range(len(PIECES)):
@@ -238,6 +224,6 @@ def tile_attend_gat_pl_tnh_k_kernel(tc, qT, kT, vT, doT, rw, qm, offs, out_0, ou
         for quad in range(4):
             queue = nc.scalar if quad % 2 else nc.sync
             queue.dma_start(
-                out=out_2[0, 4 * quad : 4 * quad + 4, :].bitcast(I32).rearrange("i (c x) -> c i x", c=CHUNKS),
+                out=out_2[0, 4 * quad : 4 * quad + 4, :].bitcast(I32).rearrange("i (s x) -> s i x", s=T // SPAN),
                 in_=out_scales[32 * quad : 32 * quad + 16, :].bitcast(I32),
             )

@@ -18,15 +18,16 @@ ALU = mybir.AluOpType
 
 P = 128
 LANES = 4
+HALF = N // 2
 RUN = 4
 
 WEAVE_SPLIT = 88
 Q_DEAL_SPLIT = 30
-DO_DEAL_SPLIT = 36
+DO_DEAL_SPLITS = (38, 26)
 
-PIECES = (512, 512, 256, 256, 256, 256)
-VECTOR_ROUNDS = 2
-VECTOR_JOINS = 3
+VECTOR_ROUNDS = 768
+VECTOR_JOINS = 1152
+LINK = 8
 STEP = 256
 SPAN = 512
 STORE_ENDS = (512, 1280, 1792, 2048)
@@ -84,8 +85,8 @@ def tile_attend_gat_pl_tnh_k_kernel(tc, qT, kT, vT, doT, rw, qm, offs, out_0, ou
                 out=bank[:],
                 lhsT=stat[0][:, cols].bitcast(stat_fmt),
                 lhsT_scale=stat[1][:, cols],
-                rhs=mov[0][:].bitcast(mov_fmt),
-                rhs_scale=mov[1][:],
+                rhs=mov[0].bitcast(mov_fmt),
+                rhs_scale=mov[1],
                 start=True,
                 stop=True,
             )
@@ -121,7 +122,7 @@ def tile_attend_gat_pl_tnh_k_kernel(tc, qT, kT, vT, doT, rw, qm, offs, out_0, ou
         slopes = []
         for t in range(LANES):
             bank = psum.tile([P, N], F32, name="score" + str(t), tag="bank" + str(t))
-            product(bank, q_mx, E4M3, t, k_mx, E4M3)
+            product(bank, q_mx, E4M3, t, (k_mx[0][:], k_mx[1][:]), E4M3)
             weight = keep.tile([P, N], F32, name="weight" + str(t))
             nc.scalar.activation(out=weight[:], in_=bank[:], func=ACT.Tanh)
             square = keep.tile([P, N], F32, name="square" + str(t))
@@ -138,89 +139,100 @@ def tile_attend_gat_pl_tnh_k_kernel(tc, qT, kT, vT, doT, rw, qm, offs, out_0, ou
         quantize(v_woven, 0, N, v_mx, E4M3, 0)
         do_mx = mx_tiles("do", R)
         do_dealt, dst, src = deal_views(do_raw, "do_dealt")
-        shared_copy(dst, src, DO_DEAL_SPLIT)
-        for t in range(LANES):
-            quantize(do_dealt, t * P, P, do_mx, E5M2, t * P)
-        ds_planes = keep.tile([P, LANES, N], BF16, name="ds_planes", align_bytes=64)
+        for pair, split in enumerate(DO_DEAL_SPLITS):
+            tiles = slice(2 * pair, 2 * pair + 2)
+            shared_copy(dst[:, :, :, :, tiles], src[:, :, :, :, tiles], split)
+        for first, count in ((0, P), (P, P), (2 * P, 2 * P)):
+            quantize(do_dealt, first, count, do_mx, E5M2, first)
+        ds_planes = keep.tile([P, LANES, N], BF16, name="ds_planes", tag="do_dealt", align_bytes=64)
         for t in range(LANES):
             bank = psum.tile([P, N], F32, name="dp" + str(t), tag="bank" + str(LANES + t))
-            product(bank, do_mx, E5M2, t, v_mx, E4M3)
-            nc.vector.scalar_tensor_tensor(
-                out=ds_planes[:, t, :], in0=bank[:], scalar=gate[:, t : t + 1], in1=slopes[t][:], op0=ALU.mult, op1=ALU.mult
-            )
-        ds_woven = weave(ds_planes, "ds_woven")
-
+            product(bank, do_mx, E5M2, t, (v_mx[0][:], v_mx[1][:]), E4M3)
+            for lo, hi in ((0, N),) if t < LANES - 1 else ((0, HALF), (HALF, N)):
+                nc.vector.scalar_tensor_tensor(
+                    out=ds_planes[:, t, lo:hi], in0=bank[:, lo:hi], scalar=gate[:, t : t + 1], in1=slopes[t][:, lo:hi], op0=ALU.mult, op1=ALU.mult
+                )
         qm_dealt, dst, src = deal_views(qm_raw, "qm_dealt")
         nc.scalar.copy(out=dst, in_=src)
-        qm_first = mx_tiles("qm_first", P, "slope" + str(LANES - 1))
-        quantize(qm_dealt, 0, P, qm_first, E4M3, 0)
-        ds_mx = mx_tiles("ds", N, "pairs")
-        quantize(ds_woven, 0, N, ds_mx, E5M2, 0)
-        qm_rest = mx_tiles("qm_rest", D - P, "ds_woven")
-        for j in range(1, LANES):
-            quantize(qm_dealt, j * P, P, qm_rest, E4M3, (j - 1) * P)
-        grads = []
+        ds_woven = keep.tile([P, N * LANES], BF16, name="ds_woven", align_bytes=64)
+        dst = ds_woven[:].rearrange("p (c i t) -> p c t i", i=RUN, t=LANES)
+        src = ds_planes[:].rearrange("p t (c i) -> p c t i", i=RUN)
+        shared_copy(dst, src, HALF // RUN)
+
+        ds_mx = mx_tiles("ds", HALF + N, "pairs")
+        nc.gpsimd.memset(ds_mx[0][:, :HALF], 0)
+        nc.gpsimd.memset(ds_mx[1][:, :HALF], 0)
+        qm_mx = mx_tiles("qm", D, "slope" + str(LANES - 1))
+        quantize(qm_dealt, 0, P, qm_mx, E4M3, 0)
+        quantize(ds_woven, 0, HALF, ds_mx, E5M2, HALF)
+        early = psum.tile([P, N], F32, name="dk_early", tag="bank" + str(LANES))
+        product(early, qm_mx, E4M3, 0, (ds_mx[0][:, :N], ds_mx[1][:, :N]), E5M2)
+        grads = [keep.tile([P, N], F32, name="grad" + str(j)) for j in range(LANES)]
+        nc.scalar.copy(out=grads[0][:, :HALF], in_=early[:, HALF:])
+        quantize(qm_dealt, P, P, qm_mx, E4M3, P)
+        quantize(qm_dealt, 2 * P, 2 * P, qm_mx, E4M3, 2 * P)
+        quantize(ds_woven, HALF, HALF, ds_mx, E5M2, N)
         for j in range(LANES):
             bank = psum.tile([P, N], F32, name="dk" + str(j), tag="bank" + str(j))
-            if j == 0:
-                product(bank, qm_first, E4M3, 0, ds_mx, E5M2)
-            else:
-                product(bank, qm_rest, E4M3, j - 1, ds_mx, E5M2)
-            grad = keep.tile([P, N], F32, name="grad" + str(j))
-            nc.scalar.copy(out=grad[:], in_=bank[:])
-            grads.append(grad)
+            product(bank, qm_mx, E4M3, j, (ds_mx[0][:, HALF:], ds_mx[1][:, HALF:]), E5M2)
+            lo = HALF if j == 0 else 0
+            nc.scalar.copy(out=grads[j][:, lo:], in_=bank[:, lo:])
 
         pairs = keep.tile([P, 2 * T * 2], BF16, name="pairs", tag="pairs", align_bytes=64)
         halves = pairs[:].rearrange("p (u n e) -> p u n e", u=2, e=2)
         pair_words = pairs[:].bitcast(F32).rearrange("p (u n) -> p u n", u=2)
-        starts = [sum(PIECES[:c]) for c in range(len(PIECES))]
-        cut = starts[VECTOR_ROUNDS]
+        cut = VECTOR_ROUNDS
         out_planes = out_0.rearrange("(p j) t -> p j t", j=LANES)
         for j in range(LANES):
-            nc.vector.tensor_copy(out=windows[j][:].indirect(offsets[:]), in_=grads[j][:])
+            for lo, hi in ((0, HALF), (HALF, N)) if j == 0 else ((0, N),):
+                nc.vector.tensor_copy(out=windows[j][:].indirect(offsets[:, lo // 16 : hi // 16]), in_=grads[j][:, lo:hi])
             nc.sync.dma_start(out=out_planes[:, j, :], in_=windows[j][:])
             if j < 2:
                 nc.scalar.copy(out=halves[:, 0, :, j], in_=windows[j][:])
             elif j == 2:
-                nc.scalar.copy(out=halves[:, 1, :cut, :], in_=windows[j][:, :cut].unsqueeze(2).to_broadcast([P, cut, 2]))
-                nc.scalar.copy(out=halves[:, 1, cut:, 0], in_=windows[j][:, cut:])
+                nc.scalar.copy(out=halves[:, 1, :cut, 0], in_=windows[j][:, :cut])
+                nc.scalar.copy(out=halves[:, 1, cut:VECTOR_JOINS, 0], in_=windows[j][:, cut:VECTOR_JOINS])
+                nc.scalar.copy(
+                    out=halves[:, 1, :cut, :].rearrange("p (h n) e -> p h n e", h=2)[:, :, :LINK, :],
+                    in_=windows[j][:, :cut].rearrange("p (h n) -> p h n", h=2)[:, :, :LINK].unsqueeze(3).to_broadcast([P, 2, LINK, 2]),
+                )
+                nc.scalar.copy(out=halves[:, 1, VECTOR_JOINS:, 0], in_=windows[j][:, VECTOR_JOINS:])
             else:
-                for c, (lo, width) in enumerate(zip(starts, PIECES)):
-                    engine_copy = nc.vector.tensor_copy if c < VECTOR_ROUNDS else nc.scalar.copy
-                    engine_copy(out=halves[:, 1, lo : lo + width, 1], in_=windows[j][:, lo : lo + width])
+                for lo, hi in ((0, cut // 2), (cut // 2, cut)):
+                    nc.vector.tensor_copy(out=halves[:, 1, lo:hi, 1], in_=windows[j][:, lo:hi])
+                for lo, hi in ((cut, VECTOR_JOINS), (VECTOR_JOINS, T - 2 * STEP), (T - 2 * STEP, T)):
+                    nc.scalar.copy(out=halves[:, 1, lo:hi, 1], in_=windows[j][:, lo:hi])
 
         out_scales = keep.tile([P, SPAN], U8, name="out_scales", align_bytes=64)
         out_words = out_1[0].rearrange("p t l -> p (t l)").bitcast(I32)
         out_codes = keep.tile([P, T], U32, name="out_codes", align_bytes=64)
-        joined = {}
+        woven = {}
 
-        def join(c):
-            lo, width = starts[c], PIECES[c]
-            tag = "kpool" if c < LANES else "vpool"
-            woven = big.tile([P, width * LANES], BF16, name="woven" + str(c), tag=tag, align_bytes=64)
-            dst = woven[:].bitcast(F32).rearrange("p (g i u) -> p g u i", i=RUN, u=2)
-            src = pair_words[:, :, lo : lo + width].rearrange("p u (g i) -> p g u i", i=RUN)
-            engine_copy = nc.vector.tensor_copy if c < VECTOR_JOINS else nc.scalar.copy
-            engine_copy(out=dst, in_=src)
-            joined[c] = woven
-
-        def emit(c):
-            for lo in range(starts[c], starts[c] + PIECES[c], STEP):
-                row, col = 4 * (lo // SPAN), lo % SPAN
-                nc.vector.quantize_mx(
-                    out=out_codes[:, lo : lo + STEP].bitcast(E4M3),
-                    scales=out_scales[row:P, col : col + STEP],
-                    in_=joined[c][:, LANES * (lo - starts[c]) : LANES * (lo - starts[c] + STEP)],
-                )
-                if lo + STEP in STORE_ENDS:
-                    first = max([0] + [end for end in STORE_ENDS if end <= lo])
-                    nc.sync.dma_start(out=out_words[:, first : lo + STEP], in_=out_codes[:, first : lo + STEP].bitcast(I32))
+        def join(first):
+            piece = keep.tile([P, STEP * LANES], BF16, name="woven" + str(first), align_bytes=64)
+            woven[first] = piece
+            for lo, hi, engine_copy in (
+                (first, min(first + STEP, VECTOR_JOINS), nc.vector.tensor_copy),
+                (max(first, VECTOR_JOINS), first + STEP, nc.scalar.copy),
+            ):
+                if lo < hi:
+                    dst = piece[:].bitcast(F32)[:, 2 * (lo - first) : 2 * (hi - first)].rearrange("p (g i u) -> p g u i", i=RUN, u=2)
+                    src = pair_words[:, :, lo:hi].rearrange("p u (g i) -> p g u i", i=RUN)
+                    engine_copy(out=dst, in_=src)
 
         join(0)
-        for c in range(len(PIECES)):
-            if c + 1 < len(PIECES):
-                join(c + 1)
-            emit(c)
+        for lo in range(0, T, STEP):
+            if lo + STEP < T:
+                join(lo + STEP)
+            row, col = 4 * (lo // SPAN), lo % SPAN
+            nc.vector.quantize_mx(
+                out=out_codes[:, lo : lo + STEP].bitcast(E4M3),
+                scales=out_scales[row:P, col : col + STEP],
+                in_=woven[lo][:],
+            )
+            if lo + STEP in STORE_ENDS:
+                first = max([0] + [end for end in STORE_ENDS if end <= lo])
+                nc.sync.dma_start(out=out_words[:, first : lo + STEP], in_=out_codes[:, first : lo + STEP].bitcast(I32))
         for quad in range(4):
             queue = nc.scalar if quad % 2 else nc.sync
             queue.dma_start(

@@ -105,15 +105,15 @@ def tile_attend_gat_pl_tnh_k_kernel(tc, qT, kT, vT, doT, rw, qm, offs, out_0, ou
         windows = []
         for j in range(LANES):
             window = keep.tile([P, T], F32, name="window" + str(j), align_bytes=64)
-            engine = nc.vector if j < LANES // 2 else nc.gpsimd
-            engine.memset(window[:].bitcast(I32), 0)
+            nc.vector.memset(window[:].bitcast(I32), 0)
             windows.append(window)
 
-        k_picked = keep.tile([P, LANES, N], BF16, name="k_picked", align_bytes=64)
+        k_woven = keep.tile([P, N * LANES], BF16, name="k_woven", align_bytes=64)
+        k_lanes = k_woven[:].rearrange("p (n j) -> p n j", j=LANES)
         for j in range(LANES):
-            nc.vector.tensor_copy(out=k_picked[:, j, :], in_=k_planes[j][:].indirect(offsets[:]))
+            nc.vector.tensor_copy(out=k_lanes[:, :, j], in_=k_planes[j][:].indirect(offsets[:]))
         k_mx = mx_tiles("k", N)
-        quantize(weave(k_picked, "k_woven"), 0, N, k_mx, E4M3, 0)
+        quantize(k_woven, 0, N, k_mx, E4M3, 0)
         q_mx = mx_tiles("q", R)
         q_dealt, dst, src = deal_views(q_raw, "q_dealt")
         shared_copy(dst, src, Q_DEAL_SPLIT)
@@ -128,15 +128,17 @@ def tile_attend_gat_pl_tnh_k_kernel(tc, qT, kT, vT, doT, rw, qm, offs, out_0, ou
             square = keep.tile([P, N], F32, name="square" + str(t))
             nc.scalar.activation(out=square[:], in_=weight[:], func=ACT.Square)
             slope = keep.tile([P, N], F32, name="slope" + str(t), align_bytes=64)
-            nc.vector.tensor_scalar(out=slope[:], in0=square[:], scalar1=-1.0, scalar2=1.0, op0=ALU.mult, op1=ALU.add)
+            nc.scalar.activation(out=slope[:], in_=square[:], func=ACT.Copy, scale=-1.0, bias=1.0)
             slopes.append(slope)
 
-        v_woven = keep.tile([P, N * LANES], BF16, name="v_woven", align_bytes=64)
+        v_woven = keep.tile([P, N * LANES], BF16, name="v_woven", tag="q_dealt", align_bytes=64)
         v_lanes = v_woven[:].rearrange("p (n j) -> p n j", j=LANES)
         for j in range(LANES):
-            nc.vector.tensor_copy(out=v_lanes[:, :, j], in_=v_planes[j][:].indirect(offsets[:]))
+            for lo, hi in ((0, N),) if j < LANES - 1 else ((0, HALF), (HALF, N)):
+                nc.vector.tensor_copy(out=v_lanes[:, lo:hi, j], in_=v_planes[j][:].indirect(offsets[:, lo // 16 : hi // 16]))
         v_mx = mx_tiles("v", N)
-        quantize(v_woven, 0, N, v_mx, E4M3, 0)
+        for lo in (0, HALF):
+            quantize(v_woven, lo, HALF, v_mx, E4M3, lo)
         do_mx = mx_tiles("do", R)
         do_dealt, dst, src = deal_views(do_raw, "do_dealt")
         for pair, split in enumerate(DO_DEAL_SPLITS):
@@ -153,15 +155,16 @@ def tile_attend_gat_pl_tnh_k_kernel(tc, qT, kT, vT, doT, rw, qm, offs, out_0, ou
                     out=ds_planes[:, t, lo:hi], in0=bank[:, lo:hi], scalar=gate[:, t : t + 1], in1=slopes[t][:, lo:hi], op0=ALU.mult, op1=ALU.mult
                 )
         qm_dealt, dst, src = deal_views(qm_raw, "qm_dealt")
-        nc.scalar.copy(out=dst, in_=src)
+        for pair in range(2):
+            nc.scalar.copy(out=dst[:, :, :, :, 2 * pair : 2 * pair + 2], in_=src[:, :, :, :, 2 * pair : 2 * pair + 2])
         ds_woven = keep.tile([P, N * LANES], BF16, name="ds_woven", align_bytes=64)
         dst = ds_woven[:].rearrange("p (c i t) -> p c t i", i=RUN, t=LANES)
         src = ds_planes[:].rearrange("p t (c i) -> p c t i", i=RUN)
         shared_copy(dst, src, HALF // RUN)
 
         ds_mx = mx_tiles("ds", HALF + N, "pairs")
-        nc.gpsimd.memset(ds_mx[0][:, :HALF], 0)
-        nc.gpsimd.memset(ds_mx[1][:, :HALF], 0)
+        nc.vector.memset(ds_mx[0][:, :HALF], 0)
+        nc.vector.memset(ds_mx[1][:, :HALF].bitcast(I32), 0)
         qm_mx = mx_tiles("qm", D, "slope" + str(LANES - 1))
         quantize(qm_dealt, 0, P, qm_mx, E4M3, 0)
         quantize(ds_woven, 0, HALF, ds_mx, E5M2, HALF)

@@ -19,6 +19,7 @@ ALU = mybir.AluOpType
 P = 128
 LANES = 4
 HALF = N // 2
+EARLY_WEAVE_SPLIT = 48
 RUN = 4
 
 WEAVE_SPLIT = 88
@@ -30,7 +31,7 @@ VECTOR_JOINS = 1152
 LINK = 8
 STEP = 256
 SPAN = 512
-STORE_ENDS = (512, 1280, 1792, 2048)
+STORE_ENDS = (768, 1280, 1792, 2048)
 
 
 def tile_attend_gat_pl_tnh_k_kernel(tc, qT, kT, vT, doT, rw, qm, offs, out_0, out_1, out_2):
@@ -96,11 +97,15 @@ def tile_attend_gat_pl_tnh_k_kernel(tc, qT, kT, vT, doT, rw, qm, offs, out_0, ou
         nc.sync.dma_start(offsets[:], offs)
         k_planes.extend(load_plane(kT, j, "kpool") for j in range(1, LANES))
         q_raw = load_square(qT, "q_raw")
-        v_planes = [load_plane(vT, j, "vpool") for j in range(LANES)]
-        do_raw = load_square(doT, "do_raw")
         gate = keep.tile([P, LANES], F32, name="gate")
         nc.sync.dma_start(out=gate[:], in_=rw[0].rearrange("(p j) o -> p (j o)", j=LANES))
-        qm_raw = load_square(qm, "qm_raw")
+        v_planes = [load_plane(vT, j, "vpool") for j in range(LANES)]
+        do_raw = load_square(doT, "do_raw")
+        qm_raw = []
+        for h in range(2):
+            raw = keep.tile([P, LANES, D // 2], F32, name="qm_raw" + str(h), align_bytes=64)
+            nc.sync.dma_start(out=raw[:], in_=qm[0].rearrange("(p j) w -> p j w", j=LANES)[:, :, h * D // 2 : (h + 1) * D // 2])
+            qm_raw.append(raw)
 
         windows = []
         for j in range(LANES):
@@ -119,6 +124,8 @@ def tile_attend_gat_pl_tnh_k_kernel(tc, qT, kT, vT, doT, rw, qm, offs, out_0, ou
         shared_copy(dst, src, Q_DEAL_SPLIT)
         for t in range(LANES):
             quantize(q_dealt, t * P, P, q_mx, E4M3, t * P)
+        negated = keep.tile([P, LANES], F32, name="negated")
+        nc.scalar.activation(out=negated[:], in_=gate[:], func=ACT.Copy, scale=-1.0)
         slopes = []
         for t in range(LANES):
             bank = psum.tile([P, N], F32, name="score" + str(t), tag="bank" + str(t))
@@ -128,7 +135,7 @@ def tile_attend_gat_pl_tnh_k_kernel(tc, qT, kT, vT, doT, rw, qm, offs, out_0, ou
             square = keep.tile([P, N], F32, name="square" + str(t))
             nc.scalar.activation(out=square[:], in_=weight[:], func=ACT.Square)
             slope = keep.tile([P, N], F32, name="slope" + str(t), align_bytes=64)
-            nc.scalar.activation(out=slope[:], in_=square[:], func=ACT.Copy, scale=-1.0, bias=1.0)
+            nc.scalar.activation(out=slope[:], in_=square[:], func=ACT.Identity, scale=negated[:, t : t + 1], bias=gate[:, t : t + 1])
             slopes.append(slope)
 
         v_woven = keep.tile([P, N * LANES], BF16, name="v_woven", tag="q_dealt", align_bytes=64)
@@ -151,16 +158,17 @@ def tile_attend_gat_pl_tnh_k_kernel(tc, qT, kT, vT, doT, rw, qm, offs, out_0, ou
             bank = psum.tile([P, N], F32, name="dp" + str(t), tag="bank" + str(LANES + t))
             product(bank, do_mx, E5M2, t, (v_mx[0][:], v_mx[1][:]), E4M3)
             for lo, hi in ((0, N),) if t < LANES - 1 else ((0, HALF), (HALF, N)):
-                nc.vector.scalar_tensor_tensor(
-                    out=ds_planes[:, t, lo:hi], in0=bank[:, lo:hi], scalar=gate[:, t : t + 1], in1=slopes[t][:, lo:hi], op0=ALU.mult, op1=ALU.mult
-                )
-        qm_dealt, dst, src = deal_views(qm_raw, "qm_dealt")
-        for pair in range(2):
-            nc.scalar.copy(out=dst[:, :, :, :, 2 * pair : 2 * pair + 2], in_=src[:, :, :, :, 2 * pair : 2 * pair + 2])
+                nc.vector.tensor_tensor(out=ds_planes[:, t, lo:hi], in0=bank[:, lo:hi], in1=slopes[t][:, lo:hi], op=ALU.mult)
+        qm_dealt = keep.tile([P, LANES * D], BF16, name="qm_dealt", align_bytes=64)
+        dst = qm_dealt[:].rearrange("p (t g h j) -> p g j h t", t=LANES, h=2, j=LANES)
+        for h in range(2):
+            src = qm_raw[h][:].rearrange("p j (g h t) -> p g j h t", h=2, t=LANES)
+            nc.scalar.copy(out=dst[:, 32 * h : 32 * h + 32], in_=src)
         ds_woven = keep.tile([P, N * LANES], BF16, name="ds_woven", align_bytes=64)
         dst = ds_woven[:].rearrange("p (c i t) -> p c t i", i=RUN, t=LANES)
         src = ds_planes[:].rearrange("p t (c i) -> p c t i", i=RUN)
-        shared_copy(dst, src, HALF // RUN)
+        shared_copy(dst[:, : HALF // RUN], src[:, : HALF // RUN], EARLY_WEAVE_SPLIT)
+        nc.scalar.copy(out=dst[:, HALF // RUN :], in_=src[:, HALF // RUN :])
 
         ds_mx = mx_tiles("ds", HALF + N, "pairs")
         nc.vector.memset(ds_mx[0][:, :HALF], 0)
@@ -216,7 +224,8 @@ def tile_attend_gat_pl_tnh_k_kernel(tc, qT, kT, vT, doT, rw, qm, offs, out_0, ou
             woven[first] = piece
             for lo, hi, engine_copy in (
                 (first, min(first + STEP, VECTOR_JOINS), nc.vector.tensor_copy),
-                (max(first, VECTOR_JOINS), first + STEP, nc.scalar.copy),
+                (max(first, VECTOR_JOINS), min(first + STEP, T - STEP // 2), nc.scalar.copy),
+                (max(first, T - STEP // 2), first + STEP, nc.scalar.copy),
             ):
                 if lo < hi:
                     dst = piece[:].bitcast(F32)[:, 2 * (lo - first) : 2 * (hi - first)].rearrange("p (g i u) -> p g u i", i=RUN, u=2)
@@ -228,14 +237,17 @@ def tile_attend_gat_pl_tnh_k_kernel(tc, qT, kT, vT, doT, rw, qm, offs, out_0, ou
             if lo + STEP < T:
                 join(lo + STEP)
             row, col = 4 * (lo // SPAN), lo % SPAN
-            nc.vector.quantize_mx(
-                out=out_codes[:, lo : lo + STEP].bitcast(E4M3),
-                scales=out_scales[row:P, col : col + STEP],
-                in_=woven[lo][:],
-            )
-            if lo + STEP in STORE_ENDS:
-                first = max([0] + [end for end in STORE_ENDS if end <= lo])
-                nc.sync.dma_start(out=out_words[:, first : lo + STEP], in_=out_codes[:, first : lo + STEP].bitcast(I32))
+            width = STEP if lo + STEP < T else STEP // 2
+            for at in range(0, STEP, width):
+                nc.vector.quantize_mx(
+                    out=out_codes[:, lo + at : lo + at + width].bitcast(E4M3),
+                    scales=out_scales[row:P, col + at : col + at + width],
+                    in_=woven[lo][:, LANES * at : LANES * (at + width)],
+                )
+                last = lo + at + width
+                if last in STORE_ENDS:
+                    first = max([0] + [end for end in STORE_ENDS if end < last])
+                    nc.sync.dma_start(out=out_words[:, first:last], in_=out_codes[:, first:last].bitcast(I32))
         for quad in range(4):
             queue = nc.scalar if quad % 2 else nc.sync
             queue.dma_start(

@@ -19,12 +19,10 @@ ALU = mybir.AluOpType
 P = 128
 LANES = 4
 HALF = N // 2
-EARLY_WEAVE_SPLIT = 48
+QUARTER = N // 4
+PAD = N - QUARTER
 RUN = 4
 
-WEAVE_SPLIT = 88
-Q_DEAL_SPLIT = 30
-DO_DEAL_SPLITS = (38, 26)
 
 VECTOR_ROUNDS = 768
 VECTOR_JOINS = 1152
@@ -51,21 +49,23 @@ def tile_attend_gat_pl_tnh_k_kernel(tc, qT, kT, vT, doT, rw, qm, offs, out_0, ou
             nc.sync.dma_start(out=raw[:], in_=src[0].rearrange("(p j) w -> p j w", j=LANES))
             return raw
 
+        def load_halves(src, name):
+            rows = src[0].rearrange("(p j) w -> p j w", j=LANES)
+            raws = []
+            for h in range(2):
+                raw = keep.tile([P, LANES, 256], F32, name=name + str(h), align_bytes=64)
+                nc.sync.dma_start(out=raw[:], in_=rows[:, :, 256 * h : 256 * (h + 1)])
+                raws.append(raw)
+            return raws
+
+        def half_views(dealt, raw, h):
+            dst = dealt[:].rearrange("p (t g h j) -> p g j h t", t=LANES, h=2, j=LANES)[:, 32 * h : 32 * h + 32]
+            return dst, raw[:].rearrange("p j (g h t) -> p g j h t", h=2, t=LANES)
+
         def mx_tiles(name, width, codes_tag=""):
             codes = keep.tile([P, width], U32, name=name + "_codes", tag=codes_tag or name + "_codes", align_bytes=64)
             scales = keep.tile([P, width], U8, name=name + "_scales", tag=name + "_scales", align_bytes=64)
             return codes, scales
-
-        def shared_copy(dst, src, split):
-            nc.vector.tensor_copy(out=dst[:, :split], in_=src[:, :split])
-            nc.scalar.copy(out=dst[:, split:], in_=src[:, split:])
-
-        def weave(planes, name):
-            woven = keep.tile([P, N * LANES], BF16, name=name, align_bytes=64)
-            dst = woven[:].rearrange("p (c i t) -> p c t i", i=RUN, t=LANES)
-            src = planes[:].rearrange("p t (c i) -> p c t i", i=RUN)
-            shared_copy(dst, src, WEAVE_SPLIT)
-            return woven
 
         def deal_views(raw, name):
             dealt = keep.tile([P, LANES * 512], BF16, name=name, align_bytes=64)
@@ -92,38 +92,33 @@ def tile_attend_gat_pl_tnh_k_kernel(tc, qT, kT, vT, doT, rw, qm, offs, out_0, ou
                 stop=True,
             )
 
-        offsets = keep.tile([P, N // 16], U16, name="offsets")
-        k_planes = [load_plane(kT, 0, "kpool")]
-        nc.sync.dma_start(offsets[:], offs)
-        k_planes.extend(load_plane(kT, j, "kpool") for j in range(1, LANES))
         q_raw = load_square(qT, "q_raw")
+        offsets = keep.tile([P, N // 16], U16, name="offsets")
+        nc.sync.dma_start(offsets[:], offs)
         gate = keep.tile([P, LANES], F32, name="gate")
-        nc.sync.dma_start(out=gate[:], in_=rw[0].rearrange("(p j) o -> p (j o)", j=LANES))
+        nc.scalar.dma_start(out=gate[:], in_=rw[0].rearrange("(p j) o -> p (j o)", j=LANES))
+        k_planes = [load_plane(kT, j, "kpool") for j in range(LANES)]
         v_planes = [load_plane(vT, j, "vpool") for j in range(LANES)]
-        do_raw = load_square(doT, "do_raw")
-        qm_raw = []
-        for h in range(2):
-            raw = keep.tile([P, LANES, D // 2], F32, name="qm_raw" + str(h), align_bytes=64)
-            nc.sync.dma_start(out=raw[:], in_=qm[0].rearrange("(p j) w -> p j w", j=LANES)[:, :, h * D // 2 : (h + 1) * D // 2])
-            qm_raw.append(raw)
+        do_raw = load_halves(doT, "do_raw")
+        qm_raw = load_halves(qm, "qm_raw")
 
         windows = []
         for j in range(LANES):
             window = keep.tile([P, T], F32, name="window" + str(j), align_bytes=64)
-            nc.vector.memset(window[:].bitcast(I32), 0)
+            engine = nc.vector if j < 2 else nc.gpsimd
+            engine.memset(window[:].bitcast(I32), 0)
             windows.append(window)
 
+        q_mx = mx_tiles("q", R)
+        q_dealt, dst, src = deal_views(q_raw, "q_dealt")
+        nc.scalar.copy(out=dst, in_=src)
+        quantize(q_dealt, 0, R, q_mx, E4M3, 0)
         k_woven = keep.tile([P, N * LANES], BF16, name="k_woven", align_bytes=64)
         k_lanes = k_woven[:].rearrange("p (n j) -> p n j", j=LANES)
         for j in range(LANES):
             nc.vector.tensor_copy(out=k_lanes[:, :, j], in_=k_planes[j][:].indirect(offsets[:]))
         k_mx = mx_tiles("k", N)
         quantize(k_woven, 0, N, k_mx, E4M3, 0)
-        q_mx = mx_tiles("q", R)
-        q_dealt, dst, src = deal_views(q_raw, "q_dealt")
-        shared_copy(dst, src, Q_DEAL_SPLIT)
-        for t in range(LANES):
-            quantize(q_dealt, t * P, P, q_mx, E4M3, t * P)
         negated = keep.tile([P, LANES], F32, name="negated")
         nc.scalar.activation(out=negated[:], in_=gate[:], func=ACT.Copy, scale=-1.0)
         slopes = []
@@ -138,7 +133,7 @@ def tile_attend_gat_pl_tnh_k_kernel(tc, qT, kT, vT, doT, rw, qm, offs, out_0, ou
             nc.scalar.activation(out=slope[:], in_=square[:], func=ACT.Identity, scale=negated[:, t : t + 1], bias=gate[:, t : t + 1])
             slopes.append(slope)
 
-        v_woven = keep.tile([P, N * LANES], BF16, name="v_woven", tag="q_dealt", align_bytes=64)
+        v_woven = keep.tile([P, N * LANES], BF16, name="v_woven", tag="k_woven", align_bytes=64)
         v_lanes = v_woven[:].rearrange("p (n j) -> p n j", j=LANES)
         for j in range(LANES):
             for lo, hi in ((0, N),) if j < LANES - 1 else ((0, HALF), (HALF, N)):
@@ -147,47 +142,83 @@ def tile_attend_gat_pl_tnh_k_kernel(tc, qT, kT, vT, doT, rw, qm, offs, out_0, ou
         for lo in (0, HALF):
             quantize(v_woven, lo, HALF, v_mx, E4M3, lo)
         do_mx = mx_tiles("do", R)
-        do_dealt, dst, src = deal_views(do_raw, "do_dealt")
-        for pair, split in enumerate(DO_DEAL_SPLITS):
-            tiles = slice(2 * pair, 2 * pair + 2)
-            shared_copy(dst[:, :, :, :, tiles], src[:, :, :, :, tiles], split)
-        for first, count in ((0, P), (P, P), (2 * P, 2 * P)):
+        do_dealt = keep.tile([P, LANES * R], BF16, name="do_dealt", align_bytes=64)
+        dst, src = half_views(do_dealt, do_raw[0], 0)
+        nc.scalar.copy(out=dst, in_=src)
+        dst, src = half_views(do_dealt, do_raw[1], 1)
+        nc.vector.tensor_copy(out=dst[:, :, :, :, :2], in_=src[:, :, :, :, :2])
+        nc.scalar.copy(out=dst[:, :, :, :, 2:], in_=src[:, :, :, :, 2:])
+        for first, count in ((0, 64), (64, 64), (P, P), (2 * P, 2 * P)):
             quantize(do_dealt, first, count, do_mx, E5M2, first)
         ds_planes = keep.tile([P, LANES, N], BF16, name="ds_planes", tag="do_dealt", align_bytes=64)
+        ds_woven = keep.tile([P, N * LANES], BF16, name="ds_woven", align_bytes=64)
+
+        def weave_ds(quarter, engine_copy):
+            runs = slice(quarter * QUARTER // RUN, (quarter + 1) * QUARTER // RUN)
+            dst = ds_woven[:].rearrange("p (c i t) -> p c t i", i=RUN, t=LANES)
+            src = ds_planes[:].rearrange("p t (c i) -> p c t i", i=RUN)
+            engine_copy(out=dst[:, runs], in_=src[:, runs])
+
         for t in range(LANES):
             bank = psum.tile([P, N], F32, name="dp" + str(t), tag="bank" + str(LANES + t))
             product(bank, do_mx, E5M2, t, (v_mx[0][:], v_mx[1][:]), E4M3)
-            for lo, hi in ((0, N),) if t < LANES - 1 else ((0, HALF), (HALF, N)):
+            for lo, hi in ((0, N),) if t < LANES - 1 else ((0, QUARTER), (QUARTER, HALF), (HALF, N)):
                 nc.vector.tensor_tensor(out=ds_planes[:, t, lo:hi], in0=bank[:, lo:hi], in1=slopes[t][:, lo:hi], op=ALU.mult)
         qm_dealt = keep.tile([P, LANES * D], BF16, name="qm_dealt", align_bytes=64)
-        dst = qm_dealt[:].rearrange("p (t g h j) -> p g j h t", t=LANES, h=2, j=LANES)
-        for h in range(2):
-            src = qm_raw[h][:].rearrange("p j (g h t) -> p g j h t", h=2, t=LANES)
-            nc.scalar.copy(out=dst[:, 32 * h : 32 * h + 32], in_=src)
-        ds_woven = keep.tile([P, N * LANES], BF16, name="ds_woven", align_bytes=64)
-        dst = ds_woven[:].rearrange("p (c i t) -> p c t i", i=RUN, t=LANES)
-        src = ds_planes[:].rearrange("p t (c i) -> p c t i", i=RUN)
-        shared_copy(dst[:, : HALF // RUN], src[:, : HALF // RUN], EARLY_WEAVE_SPLIT)
-        nc.scalar.copy(out=dst[:, HALF // RUN :], in_=src[:, HALF // RUN :])
 
-        ds_mx = mx_tiles("ds", HALF + N, "pairs")
-        nc.vector.memset(ds_mx[0][:, :HALF], 0)
-        nc.vector.memset(ds_mx[1][:, :HALF].bitcast(I32), 0)
+        def deal_qm(h, tiles):
+            dst, src = half_views(qm_dealt, qm_raw[h], h)
+            nc.scalar.copy(out=dst[:, :, :, :, tiles], in_=src[:, :, :, :, tiles])
+
+        deal_qm(0, slice(0, 4))
+        deal_qm(1, slice(0, 2))
+        ds_mx = mx_tiles("ds", PAD + N, "pairs")
+        nc.vector.memset(ds_mx[0][:, :PAD], 0)
+        nc.vector.memset(ds_mx[1][:, :PAD].bitcast(I32), 0)
+        zeros = keep.tile([P, QUARTER], F32, name="zeros", align_bytes=64)
+        nc.vector.memset(zeros[:], 0.0)
         qm_mx = mx_tiles("qm", D, "slope" + str(LANES - 1))
-        quantize(qm_dealt, 0, P, qm_mx, E4M3, 0)
-        quantize(ds_woven, 0, HALF, ds_mx, E5M2, HALF)
-        early = psum.tile([P, N], F32, name="dk_early", tag="bank" + str(LANES))
-        product(early, qm_mx, E4M3, 0, (ds_mx[0][:, :N], ds_mx[1][:, :N]), E5M2)
         grads = [keep.tile([P, N], F32, name="grad" + str(j)) for j in range(LANES)]
-        nc.scalar.copy(out=grads[0][:, :HALF], in_=early[:, HALF:])
-        quantize(qm_dealt, P, P, qm_mx, E4M3, P)
-        quantize(qm_dealt, 2 * P, 2 * P, qm_mx, E4M3, 2 * P)
-        quantize(ds_woven, HALF, HALF, ds_mx, E5M2, N)
-        for j in range(LANES):
+
+        def early_pass(quarter):
+            cols = slice(quarter * QUARTER, quarter * QUARTER + N)
+            bank = psum.tile([P, N], F32, name="early" + str(quarter), tag="bank" + str(LANES + quarter))
+            product(bank, qm_mx, E4M3, 0, (ds_mx[0][:, cols], ds_mx[1][:, cols]), E5M2)
+            nc.scalar.copy(out=grads[0][:, quarter * QUARTER : (quarter + 1) * QUARTER], in_=bank[:, PAD:])
+
+        def scatter_quarter(quarter):
+            lo, hi = quarter * QUARTER, (quarter + 1) * QUARTER
+            nc.vector.tensor_tensor(out=windows[0][:].indirect(offsets[:, lo // 16 : hi // 16]), in0=grads[0][:, lo:hi], in1=zeros[:], op=ALU.add)
+
+        weave_ds(0, nc.scalar.copy)
+        quantize(qm_dealt, 0, 2 * P, qm_mx, E4M3, 0)
+        quantize(ds_woven, 0, QUARTER, ds_mx, E5M2, PAD)
+        early_pass(0)
+        weave_ds(1, nc.vector.tensor_copy)
+        weave_ds(2, nc.scalar.copy)
+        weave_ds(3, nc.scalar.copy)
+        quantize(ds_woven, QUARTER, QUARTER, ds_mx, E5M2, PAD + QUARTER)
+        early_pass(1)
+        scatter_quarter(0)
+        quantize(ds_woven, HALF, HALF, ds_mx, E5M2, PAD + HALF)
+        scatter_quarter(1)
+
+        def dk_pass(j, lo):
             bank = psum.tile([P, N], F32, name="dk" + str(j), tag="bank" + str(j))
-            product(bank, qm_mx, E4M3, j, (ds_mx[0][:, HALF:], ds_mx[1][:, HALF:]), E5M2)
-            lo = HALF if j == 0 else 0
+            product(bank, qm_mx, E4M3, j, (ds_mx[0][:, PAD:], ds_mx[1][:, PAD:]), E5M2)
             nc.scalar.copy(out=grads[j][:, lo:], in_=bank[:, lo:])
+
+        dk_pass(0, HALF)
+        qm_late = keep.tile([P, 2 * 64 * LANES], BF16, name="qm_late", tag="do_dealt", align_bytes=64)
+        nc.scalar.copy(
+            out=qm_late[:].rearrange("p (t g h j) -> p g j h t", t=2, h=2, j=LANES),
+            in_=qm_raw[1][:].rearrange("p j (g h t) -> p g j h t", h=2, t=LANES)[:, :, :, :, 2:],
+        )
+        for t in (2, 3):
+            quantize(qm_dealt, t * P, 64, qm_mx, E4M3, t * P)
+            quantize(qm_late, (t - 2) * 64, 64, qm_mx, E4M3, t * P + 64)
+        for j in range(1, LANES):
+            dk_pass(j, 0)
 
         pairs = keep.tile([P, 2 * T * 2], BF16, name="pairs", tag="pairs", align_bytes=64)
         halves = pairs[:].rearrange("p (u n e) -> p u n e", u=2, e=2)
@@ -195,8 +226,8 @@ def tile_attend_gat_pl_tnh_k_kernel(tc, qT, kT, vT, doT, rw, qm, offs, out_0, ou
         cut = VECTOR_ROUNDS
         out_planes = out_0.rearrange("(p j) t -> p j t", j=LANES)
         for j in range(LANES):
-            for lo, hi in ((0, HALF), (HALF, N)) if j == 0 else ((0, N),):
-                nc.vector.tensor_copy(out=windows[j][:].indirect(offsets[:, lo // 16 : hi // 16]), in_=grads[j][:, lo:hi])
+            lo = HALF if j == 0 else 0
+            nc.vector.tensor_copy(out=windows[j][:].indirect(offsets[:, lo // 16 :]), in_=grads[j][:, lo:])
             nc.sync.dma_start(out=out_planes[:, j, :], in_=windows[j][:])
             if j < 2:
                 nc.scalar.copy(out=halves[:, 0, :, j], in_=windows[j][:])

@@ -19,8 +19,7 @@ ALU = mybir.AluOpType
 P = 128
 LANES = 4
 HALF = N // 2
-QUARTER = N // 4
-PAD = N - QUARTER
+EARLY_WEAVE_SPLIT = 48
 RUN = 4
 
 
@@ -66,6 +65,10 @@ def tile_attend_gat_pl_tnh_k_kernel(tc, qT, kT, vT, doT, rw, qm, offs, out_0, ou
             codes = keep.tile([P, width], U32, name=name + "_codes", tag=codes_tag or name + "_codes", align_bytes=64)
             scales = keep.tile([P, width], U8, name=name + "_scales", tag=name + "_scales", align_bytes=64)
             return codes, scales
+
+        def shared_copy(dst, src, split):
+            nc.vector.tensor_copy(out=dst[:, :split], in_=src[:, :split])
+            nc.scalar.copy(out=dst[:, split:], in_=src[:, split:])
 
         def deal_views(raw, name):
             dealt = keep.tile([P, LANES * 512], BF16, name=name, align_bytes=64)
@@ -151,74 +154,39 @@ def tile_attend_gat_pl_tnh_k_kernel(tc, qT, kT, vT, doT, rw, qm, offs, out_0, ou
         for first, count in ((0, 64), (64, 64), (P, P), (2 * P, 2 * P)):
             quantize(do_dealt, first, count, do_mx, E5M2, first)
         ds_planes = keep.tile([P, LANES, N], BF16, name="ds_planes", tag="do_dealt", align_bytes=64)
-        ds_woven = keep.tile([P, N * LANES], BF16, name="ds_woven", align_bytes=64)
-
-        def weave_ds(quarter, engine_copy):
-            runs = slice(quarter * QUARTER // RUN, (quarter + 1) * QUARTER // RUN)
-            dst = ds_woven[:].rearrange("p (c i t) -> p c t i", i=RUN, t=LANES)
-            src = ds_planes[:].rearrange("p t (c i) -> p c t i", i=RUN)
-            engine_copy(out=dst[:, runs], in_=src[:, runs])
-
         for t in range(LANES):
             bank = psum.tile([P, N], F32, name="dp" + str(t), tag="bank" + str(LANES + t))
             product(bank, do_mx, E5M2, t, (v_mx[0][:], v_mx[1][:]), E4M3)
-            for lo, hi in ((0, N),) if t < LANES - 1 else ((0, QUARTER), (QUARTER, HALF), (HALF, N)):
+            for lo, hi in ((0, N),) if t < LANES - 1 else ((0, HALF), (HALF, N)):
                 nc.vector.tensor_tensor(out=ds_planes[:, t, lo:hi], in0=bank[:, lo:hi], in1=slopes[t][:, lo:hi], op=ALU.mult)
         qm_dealt = keep.tile([P, LANES * D], BF16, name="qm_dealt", align_bytes=64)
-
-        def deal_qm(h, tiles):
+        for h in range(2):
             dst, src = half_views(qm_dealt, qm_raw[h], h)
-            nc.scalar.copy(out=dst[:, :, :, :, tiles], in_=src[:, :, :, :, tiles])
+            nc.scalar.copy(out=dst, in_=src)
+        ds_woven = keep.tile([P, N * LANES], BF16, name="ds_woven", align_bytes=64)
+        dst = ds_woven[:].rearrange("p (c i t) -> p c t i", i=RUN, t=LANES)
+        src = ds_planes[:].rearrange("p t (c i) -> p c t i", i=RUN)
+        shared_copy(dst[:, : HALF // RUN], src[:, : HALF // RUN], EARLY_WEAVE_SPLIT)
+        nc.scalar.copy(out=dst[:, HALF // RUN :], in_=src[:, HALF // RUN :])
 
-        deal_qm(0, slice(0, 4))
-        deal_qm(1, slice(0, 2))
-        ds_mx = mx_tiles("ds", PAD + N, "pairs")
-        nc.vector.memset(ds_mx[0][:, :PAD], 0)
-        nc.vector.memset(ds_mx[1][:, :PAD].bitcast(I32), 0)
-        zeros = keep.tile([P, QUARTER], F32, name="zeros", align_bytes=64)
-        nc.vector.memset(zeros[:], 0.0)
+        ds_mx = mx_tiles("ds", HALF + N, "pairs")
+        nc.vector.memset(ds_mx[0][:, :HALF], 0)
+        nc.vector.memset(ds_mx[1][:, :HALF].bitcast(I32), 0)
         qm_mx = mx_tiles("qm", D, "slope" + str(LANES - 1))
+        quantize(qm_dealt, 0, P, qm_mx, E4M3, 0)
+        quantize(ds_woven, 0, HALF, ds_mx, E5M2, HALF)
+        early = psum.tile([P, N], F32, name="dk_early", tag="bank" + str(LANES))
+        product(early, qm_mx, E4M3, 0, (ds_mx[0][:, :N], ds_mx[1][:, :N]), E5M2)
         grads = [keep.tile([P, N], F32, name="grad" + str(j)) for j in range(LANES)]
-
-        def early_pass(quarter):
-            cols = slice(quarter * QUARTER, quarter * QUARTER + N)
-            bank = psum.tile([P, N], F32, name="early" + str(quarter), tag="bank" + str(LANES + quarter))
-            product(bank, qm_mx, E4M3, 0, (ds_mx[0][:, cols], ds_mx[1][:, cols]), E5M2)
-            nc.scalar.copy(out=grads[0][:, quarter * QUARTER : (quarter + 1) * QUARTER], in_=bank[:, PAD:])
-
-        def scatter_quarter(quarter):
-            lo, hi = quarter * QUARTER, (quarter + 1) * QUARTER
-            nc.vector.tensor_tensor(out=windows[0][:].indirect(offsets[:, lo // 16 : hi // 16]), in0=grads[0][:, lo:hi], in1=zeros[:], op=ALU.add)
-
-        weave_ds(0, nc.scalar.copy)
-        quantize(qm_dealt, 0, 2 * P, qm_mx, E4M3, 0)
-        quantize(ds_woven, 0, QUARTER, ds_mx, E5M2, PAD)
-        early_pass(0)
-        weave_ds(1, nc.vector.tensor_copy)
-        weave_ds(2, nc.scalar.copy)
-        weave_ds(3, nc.scalar.copy)
-        quantize(ds_woven, QUARTER, QUARTER, ds_mx, E5M2, PAD + QUARTER)
-        early_pass(1)
-        scatter_quarter(0)
-        quantize(ds_woven, HALF, HALF, ds_mx, E5M2, PAD + HALF)
-        scatter_quarter(1)
-
-        def dk_pass(j, lo):
+        nc.scalar.copy(out=grads[0][:, :HALF], in_=early[:, HALF:])
+        quantize(qm_dealt, P, P, qm_mx, E4M3, P)
+        quantize(qm_dealt, 2 * P, 2 * P, qm_mx, E4M3, 2 * P)
+        quantize(ds_woven, HALF, HALF, ds_mx, E5M2, N)
+        for j in range(LANES):
             bank = psum.tile([P, N], F32, name="dk" + str(j), tag="bank" + str(j))
-            product(bank, qm_mx, E4M3, j, (ds_mx[0][:, PAD:], ds_mx[1][:, PAD:]), E5M2)
+            product(bank, qm_mx, E4M3, j, (ds_mx[0][:, HALF:], ds_mx[1][:, HALF:]), E5M2)
+            lo = HALF if j == 0 else 0
             nc.scalar.copy(out=grads[j][:, lo:], in_=bank[:, lo:])
-
-        dk_pass(0, HALF)
-        qm_late = keep.tile([P, 2 * 64 * LANES], BF16, name="qm_late", tag="do_dealt", align_bytes=64)
-        nc.scalar.copy(
-            out=qm_late[:].rearrange("p (t g h j) -> p g j h t", t=2, h=2, j=LANES),
-            in_=qm_raw[1][:].rearrange("p j (g h t) -> p g j h t", h=2, t=LANES)[:, :, :, :, 2:],
-        )
-        for t in (2, 3):
-            quantize(qm_dealt, t * P, 64, qm_mx, E4M3, t * P)
-            quantize(qm_late, (t - 2) * 64, 64, qm_mx, E4M3, t * P + 64)
-        for j in range(1, LANES):
-            dk_pass(j, 0)
 
         pairs = keep.tile([P, 2 * T * 2], BF16, name="pairs", tag="pairs", align_bytes=64)
         halves = pairs[:].rearrange("p (u n e) -> p u n e", u=2, e=2)
@@ -226,8 +194,8 @@ def tile_attend_gat_pl_tnh_k_kernel(tc, qT, kT, vT, doT, rw, qm, offs, out_0, ou
         cut = VECTOR_ROUNDS
         out_planes = out_0.rearrange("(p j) t -> p j t", j=LANES)
         for j in range(LANES):
-            lo = HALF if j == 0 else 0
-            nc.vector.tensor_copy(out=windows[j][:].indirect(offsets[:, lo // 16 :]), in_=grads[j][:, lo:])
+            for lo, hi in ((0, HALF), (HALF, N)) if j == 0 else ((0, N),):
+                nc.vector.tensor_copy(out=windows[j][:].indirect(offsets[:, lo // 16 : hi // 16]), in_=grads[j][:, lo:hi])
             nc.sync.dma_start(out=out_planes[:, j, :], in_=windows[j][:])
             if j < 2:
                 nc.scalar.copy(out=halves[:, 0, :, j], in_=windows[j][:])

@@ -23,6 +23,8 @@ EARLY_WEAVE_SPLIT = 48
 RUN = 4
 
 
+DO_DEAL_SPLITS = (42, 30)
+
 VECTOR_ROUNDS = 768
 VECTOR_JOINS = 1152
 LINK = 8
@@ -35,11 +37,10 @@ def tile_attend_gat_pl_tnh_k_kernel(tc, qT, kT, vT, doT, rw, qm, offs, out_0, ou
     nc = tc.nc
     with ExitStack() as ctx:
         keep = ctx.enter_context(tc.tile_pool(name="keep", bufs=1))
-        big = ctx.enter_context(tc.tile_pool(name="big", bufs=LANES))
         psum = ctx.enter_context(tc.psum_pool(name="psum", bufs=1))
 
         def load_plane(src, j, tag):
-            plane = big.tile([P, T], F32, name=tag + str(j), tag=tag, align_bytes=64)
+            plane = keep.tile([P, T], F32, name=tag + str(j), align_bytes=64)
             nc.sync.dma_start(out=plane[:], in_=src.rearrange("(p j) t -> p j t", j=LANES)[:, j, :])
             return plane
 
@@ -100,9 +101,11 @@ def tile_attend_gat_pl_tnh_k_kernel(tc, qT, kT, vT, doT, rw, qm, offs, out_0, ou
         nc.sync.dma_start(offsets[:], offs)
         gate = keep.tile([P, LANES], F32, name="gate")
         nc.scalar.dma_start(out=gate[:], in_=rw[0].rearrange("(p j) o -> p (j o)", j=LANES))
-        k_planes = [load_plane(kT, j, "kpool") for j in range(LANES)]
+        k_first = keep.tile([P, 2, T], F32, name="k_first", align_bytes=64)
+        nc.sync.dma_start(out=k_first[:], in_=kT.rearrange("(p j) t -> p j t", j=LANES)[:, :2, :])
+        k_planes = [k_first[:, 0, :], k_first[:, 1, :]] + [load_plane(kT, j, "kpool")[:] for j in (2, 3)]
         v_planes = [load_plane(vT, j, "vpool") for j in range(LANES)]
-        do_raw = load_halves(doT, "do_raw")
+        do_raw = load_square(doT, "do_raw")
         qm_raw = load_halves(qm, "qm_raw")
 
         windows = []
@@ -119,7 +122,7 @@ def tile_attend_gat_pl_tnh_k_kernel(tc, qT, kT, vT, doT, rw, qm, offs, out_0, ou
         k_woven = keep.tile([P, N * LANES], BF16, name="k_woven", align_bytes=64)
         k_lanes = k_woven[:].rearrange("p (n j) -> p n j", j=LANES)
         for j in range(LANES):
-            nc.vector.tensor_copy(out=k_lanes[:, :, j], in_=k_planes[j][:].indirect(offsets[:]))
+            nc.vector.tensor_copy(out=k_lanes[:, :, j], in_=k_planes[j].indirect(offsets[:]))
         k_mx = mx_tiles("k", N)
         quantize(k_woven, 0, N, k_mx, E4M3, 0)
         negated = keep.tile([P, LANES], F32, name="negated")
@@ -145,13 +148,11 @@ def tile_attend_gat_pl_tnh_k_kernel(tc, qT, kT, vT, doT, rw, qm, offs, out_0, ou
         for lo in (0, HALF):
             quantize(v_woven, lo, HALF, v_mx, E4M3, lo)
         do_mx = mx_tiles("do", R)
-        do_dealt = keep.tile([P, LANES * R], BF16, name="do_dealt", align_bytes=64)
-        dst, src = half_views(do_dealt, do_raw[0], 0)
-        nc.scalar.copy(out=dst, in_=src)
-        dst, src = half_views(do_dealt, do_raw[1], 1)
-        nc.vector.tensor_copy(out=dst[:, :, :, :, :2], in_=src[:, :, :, :, :2])
-        nc.scalar.copy(out=dst[:, :, :, :, 2:], in_=src[:, :, :, :, 2:])
-        for first, count in ((0, 64), (64, 64), (P, P), (2 * P, 2 * P)):
+        do_dealt, dst, src = deal_views(do_raw, "do_dealt")
+        for pair, split in enumerate(DO_DEAL_SPLITS):
+            tiles = slice(2 * pair, 2 * pair + 2)
+            shared_copy(dst[:, :, :, :, tiles], src[:, :, :, :, tiles], split)
+        for first, count in ((0, P), (P, P), (2 * P, 2 * P)):
             quantize(do_dealt, first, count, do_mx, E5M2, first)
         ds_planes = keep.tile([P, LANES, N], BF16, name="ds_planes", tag="do_dealt", align_bytes=64)
         for t in range(LANES):

@@ -19,11 +19,11 @@ ALU = mybir.AluOpType
 P = 128
 LANES = 4
 HALF = N // 2
-EARLY_WEAVE_SPLIT = 48
+EARLY_WEAVE_SPLIT = 40
 RUN = 4
 
 
-DO_DEAL_SPLITS = (42, 30)
+DO_DEAL_SPLITS = (36, 30)
 
 VECTOR_ROUNDS = 768
 VECTOR_JOINS = 1152
@@ -161,9 +161,17 @@ def tile_attend_gat_pl_tnh_k_kernel(tc, qT, kT, vT, doT, rw, qm, offs, out_0, ou
             for lo, hi in ((0, N),) if t < LANES - 1 else ((0, HALF), (HALF, N)):
                 nc.vector.tensor_tensor(out=ds_planes[:, t, lo:hi], in0=bank[:, lo:hi], in1=slopes[t][:, lo:hi], op=ALU.mult)
         qm_dealt = keep.tile([P, LANES * D], BF16, name="qm_dealt", align_bytes=64)
-        for h in range(2):
+        for h, tiles in ((0, slice(0, LANES)), (1, slice(0, 2))):
             dst, src = half_views(qm_dealt, qm_raw[h], h)
-            nc.scalar.copy(out=dst, in_=src)
+            nc.scalar.copy(out=dst[:, :, :, :, tiles], in_=src[:, :, :, :, tiles])
+        nc.gpsimd.tensor_scalar(
+            out=qm_dealt[:].rearrange("p (t m j) -> p m j t", t=LANES, j=LANES)[:, 64:, :, 2:],
+            in0=qm_raw[1][:].rearrange("p j (m t) -> p m j t", t=LANES)[:, :, :, 2:],
+            scalar1=1.0,
+            scalar2=0.0,
+            op0=ALU.mult,
+            op1=ALU.add,
+        )
         ds_woven = keep.tile([P, N * LANES], BF16, name="ds_woven", align_bytes=64)
         dst = ds_woven[:].rearrange("p (c i t) -> p c t i", i=RUN, t=LANES)
         src = ds_planes[:].rearrange("p t (c i) -> p c t i", i=RUN)

@@ -19,18 +19,11 @@ ALU = mybir.AluOpType
 P = 128
 LANES = 4
 HALF = N // 2
-EARLY_WEAVE_SPLIT = 40
+CHUNK = 128
 RUN = 4
-
-
 DO_DEAL_SPLITS = (36, 30)
-
-VECTOR_ROUNDS = 768
-VECTOR_JOINS = 1152
-LINK = 8
 STEP = 256
 SPAN = 512
-STORE_ENDS = (768, 1280, 1792, 2048)
 
 
 def tile_attend_gat_pl_tnh_k_kernel(tc, qT, kT, vT, doT, rw, qm, offs, out_0, out_1, out_2):
@@ -62,9 +55,9 @@ def tile_attend_gat_pl_tnh_k_kernel(tc, qT, kT, vT, doT, rw, qm, offs, out_0, ou
             dst = dealt[:].rearrange("p (t g h j) -> p g j h t", t=LANES, h=2, j=LANES)[:, 32 * h : 32 * h + 32]
             return dst, raw[:].rearrange("p j (g h t) -> p g j h t", h=2, t=LANES)
 
-        def mx_tiles(name, width, codes_tag=""):
-            codes = keep.tile([P, width], U32, name=name + "_codes", tag=codes_tag or name + "_codes", align_bytes=64)
-            scales = keep.tile([P, width], U8, name=name + "_scales", tag=name + "_scales", align_bytes=64)
+        def mx_tiles(name, width):
+            codes = keep.tile([P, width], U32, name=name + "_codes", align_bytes=64)
+            scales = keep.tile([P, width], U8, name=name + "_scales", align_bytes=64)
             return codes, scales
 
         def shared_copy(dst, src, split):
@@ -84,14 +77,14 @@ def tile_attend_gat_pl_tnh_k_kernel(tc, qT, kT, vT, doT, rw, qm, offs, out_0, ou
                 in_=src[:, LANES * first : LANES * (first + count)],
             )
 
-        def product(bank, stat, stat_fmt, tile, mov, mov_fmt):
+        def product(out, stat, stat_fmt, tile, mov, mov_fmt, lo, hi):
             cols = slice(tile * P, (tile + 1) * P)
             nc.tensor.matmul_mx(
-                out=bank[:],
+                out=out,
                 lhsT=stat[0][:, cols].bitcast(stat_fmt),
                 lhsT_scale=stat[1][:, cols],
-                rhs=mov[0].bitcast(mov_fmt),
-                rhs_scale=mov[1],
+                rhs=mov[0][:, lo:hi].bitcast(mov_fmt),
+                rhs_scale=mov[1][:, lo:hi],
                 start=True,
                 stop=True,
             )
@@ -101,12 +94,15 @@ def tile_attend_gat_pl_tnh_k_kernel(tc, qT, kT, vT, doT, rw, qm, offs, out_0, ou
         nc.sync.dma_start(offsets[:], offs)
         gate = keep.tile([P, LANES], F32, name="gate")
         nc.scalar.dma_start(out=gate[:], in_=rw[0].rearrange("(p j) o -> p (j o)", j=LANES))
-        k_first = keep.tile([P, 2, T], F32, name="k_first", align_bytes=64)
+        k_first = keep.tile([P, 2, T], F32, name="k_first", tag="k_first", align_bytes=64)
         nc.sync.dma_start(out=k_first[:], in_=kT.rearrange("(p j) t -> p j t", j=LANES)[:, :2, :])
         k_planes = [k_first[:, 0, :], k_first[:, 1, :]] + [load_plane(kT, j, "kpool")[:] for j in (2, 3)]
         v_planes = [load_plane(vT, j, "vpool") for j in range(LANES)]
         do_raw = load_square(doT, "do_raw")
         qm_raw = load_halves(qm, "qm_raw")
+
+        def listed(lo, hi):
+            return offsets[:, lo // 16 : hi // 16]
 
         windows = []
         for j in range(LANES):
@@ -119,7 +115,7 @@ def tile_attend_gat_pl_tnh_k_kernel(tc, qT, kT, vT, doT, rw, qm, offs, out_0, ou
         q_dealt, dst, src = deal_views(q_raw, "q_dealt")
         nc.scalar.copy(out=dst, in_=src)
         quantize(q_dealt, 0, R, q_mx, E4M3, 0)
-        k_woven = keep.tile([P, N * LANES], BF16, name="k_woven", align_bytes=64)
+        k_woven = keep.tile([P, N * LANES], BF16, name="k_woven", tag="k_woven", align_bytes=64)
         k_lanes = k_woven[:].rearrange("p (n j) -> p n j", j=LANES)
         for j in range(LANES):
             nc.vector.tensor_copy(out=k_lanes[:, :, j], in_=k_planes[j].indirect(offsets[:]))
@@ -127,23 +123,21 @@ def tile_attend_gat_pl_tnh_k_kernel(tc, qT, kT, vT, doT, rw, qm, offs, out_0, ou
         quantize(k_woven, 0, N, k_mx, E4M3, 0)
         negated = keep.tile([P, LANES], F32, name="negated")
         nc.scalar.activation(out=negated[:], in_=gate[:], func=ACT.Copy, scale=-1.0)
-        slopes = []
+        slopes = keep.tile([P, LANES, N], F32, name="slopes", align_bytes=64)
         for t in range(LANES):
             bank = psum.tile([P, N], F32, name="score" + str(t), tag="bank" + str(t))
-            product(bank, q_mx, E4M3, t, (k_mx[0][:], k_mx[1][:]), E4M3)
+            product(bank[:], q_mx, E4M3, t, k_mx, E4M3, 0, N)
             weight = keep.tile([P, N], F32, name="weight" + str(t))
             nc.scalar.activation(out=weight[:], in_=bank[:], func=ACT.Tanh)
             square = keep.tile([P, N], F32, name="square" + str(t))
             nc.scalar.activation(out=square[:], in_=weight[:], func=ACT.Square)
-            slope = keep.tile([P, N], F32, name="slope" + str(t), align_bytes=64)
-            nc.scalar.activation(out=slope[:], in_=square[:], func=ACT.Identity, scale=negated[:, t : t + 1], bias=gate[:, t : t + 1])
-            slopes.append(slope)
+            nc.scalar.activation(out=slopes[:, t, :], in_=square[:], func=ACT.Identity, scale=negated[:, t : t + 1], bias=gate[:, t : t + 1])
 
         v_woven = keep.tile([P, N * LANES], BF16, name="v_woven", tag="k_woven", align_bytes=64)
         v_lanes = v_woven[:].rearrange("p (n j) -> p n j", j=LANES)
         for j in range(LANES):
             for lo, hi in ((0, N),) if j < LANES - 1 else ((0, HALF), (HALF, N)):
-                nc.vector.tensor_copy(out=v_lanes[:, lo:hi, j], in_=v_planes[j][:].indirect(offsets[:, lo // 16 : hi // 16]))
+                nc.vector.tensor_copy(out=v_lanes[:, lo:hi, j], in_=v_planes[j][:].indirect(listed(lo, hi)))
         v_mx = mx_tiles("v", N)
         for lo in (0, HALF):
             quantize(v_woven, lo, HALF, v_mx, E4M3, lo)
@@ -152,110 +146,120 @@ def tile_attend_gat_pl_tnh_k_kernel(tc, qT, kT, vT, doT, rw, qm, offs, out_0, ou
         for pair, split in enumerate(DO_DEAL_SPLITS):
             tiles = slice(2 * pair, 2 * pair + 2)
             shared_copy(dst[:, :, :, :, tiles], src[:, :, :, :, tiles], split)
-        for first, count in ((0, P), (P, P), (2 * P, 2 * P)):
-            quantize(do_dealt, first, count, do_mx, E5M2, first)
-        ds_planes = keep.tile([P, LANES, N], BF16, name="ds_planes", tag="do_dealt", align_bytes=64)
-        for t in range(LANES):
-            bank = psum.tile([P, N], F32, name="dp" + str(t), tag="bank" + str(LANES + t))
-            product(bank, do_mx, E5M2, t, (v_mx[0][:], v_mx[1][:]), E4M3)
-            for lo, hi in ((0, N),) if t < LANES - 1 else ((0, HALF), (HALF, N)):
-                nc.vector.tensor_tensor(out=ds_planes[:, t, lo:hi], in0=bank[:, lo:hi], in1=slopes[t][:, lo:hi], op=ALU.mult)
+        for first in (0, 2 * P):
+            quantize(do_dealt, first, 2 * P, do_mx, E5M2, first)
         qm_dealt = keep.tile([P, LANES * D], BF16, name="qm_dealt", align_bytes=64)
-        for h, tiles in ((0, slice(0, LANES)), (1, slice(0, 2))):
+        for h, tiles in ((0, slice(0, LANES)), (1, slice(0, 2)), (1, slice(2, LANES))):
             dst, src = half_views(qm_dealt, qm_raw[h], h)
             nc.scalar.copy(out=dst[:, :, :, :, tiles], in_=src[:, :, :, :, tiles])
-        nc.gpsimd.tensor_scalar(
-            out=qm_dealt[:].rearrange("p (t m j) -> p m j t", t=LANES, j=LANES)[:, 64:, :, 2:],
-            in0=qm_raw[1][:].rearrange("p j (m t) -> p m j t", t=LANES)[:, :, :, 2:],
-            scalar1=1.0,
-            scalar2=0.0,
-            op0=ALU.mult,
-            op1=ALU.add,
-        )
-        ds_woven = keep.tile([P, N * LANES], BF16, name="ds_woven", align_bytes=64)
-        dst = ds_woven[:].rearrange("p (c i t) -> p c t i", i=RUN, t=LANES)
-        src = ds_planes[:].rearrange("p t (c i) -> p c t i", i=RUN)
-        shared_copy(dst[:, : HALF // RUN], src[:, : HALF // RUN], EARLY_WEAVE_SPLIT)
-        nc.scalar.copy(out=dst[:, HALF // RUN :], in_=src[:, HALF // RUN :])
 
-        ds_mx = mx_tiles("ds", HALF + N, "pairs")
-        nc.vector.memset(ds_mx[0][:, :HALF], 0)
-        nc.vector.memset(ds_mx[1][:, :HALF].bitcast(I32), 0)
-        qm_mx = mx_tiles("qm", D, "slope" + str(LANES - 1))
-        quantize(qm_dealt, 0, P, qm_mx, E4M3, 0)
-        quantize(ds_woven, 0, HALF, ds_mx, E5M2, HALF)
-        early = psum.tile([P, N], F32, name="dk_early", tag="bank" + str(LANES))
-        product(early, qm_mx, E4M3, 0, (ds_mx[0][:, :N], ds_mx[1][:, :N]), E5M2)
-        grads = [keep.tile([P, N], F32, name="grad" + str(j)) for j in range(LANES)]
-        nc.scalar.copy(out=grads[0][:, :HALF], in_=early[:, HALF:])
-        quantize(qm_dealt, P, P, qm_mx, E4M3, P)
-        quantize(qm_dealt, 2 * P, 2 * P, qm_mx, E4M3, 2 * P)
-        quantize(ds_woven, HALF, HALF, ds_mx, E5M2, N)
-        for j in range(LANES):
-            bank = psum.tile([P, N], F32, name="dk" + str(j), tag="bank" + str(j))
-            product(bank, qm_mx, E4M3, j, (ds_mx[0][:, HALF:], ds_mx[1][:, HALF:]), E5M2)
-            lo = HALF if j == 0 else 0
-            nc.scalar.copy(out=grads[j][:, lo:], in_=bank[:, lo:])
+        ds_mx = mx_tiles("ds", N)
+        qm_mx = mx_tiles("qm", D)
 
-        pairs = keep.tile([P, 2 * T * 2], BF16, name="pairs", tag="pairs", align_bytes=64)
+        def gradient(j, lo, hi, bank_number):
+            bank = psum.tile([P, hi - lo], F32, name="dk%d_%d" % (j, lo), tag="bank" + str(bank_number))
+            product(bank[:], qm_mx, E4M3, j, ds_mx, E5M2, lo, hi)
+            return bank
+
+        def emptied(bank, name):
+            grad = keep.tile([P, bank.shape[1]], F32, name=name)
+            nc.scalar.copy(out=grad[:], in_=bank[:])
+            return grad
+
+        def vector_scatter(j, lo, values):
+            nc.vector.tensor_copy(out=windows[j][:].indirect(listed(lo, lo + HALF)), in_=values)
+
+        def scalar_scatter(j, lo, values):
+            nc.scalar.activation(out=windows[j][:].indirect(listed(lo, lo + HALF)), in_=values, func=ACT.Copy)
+
+        first_banks = {}
+        for h in range(2):
+            ds_woven = keep.tile([P, HALF * LANES], BF16, name="ds_woven" + str(h), align_bytes=64)
+            for c in range(2):
+                lo = h * HALF + c * CHUNK
+                bank = psum.tile([P, LANES, CHUNK], F32, name="dp" + str(lo), tag="bank" + str(LANES + lo // CHUNK))
+                for t in range(LANES):
+                    product(bank[:, t, :], do_mx, E5M2, t, v_mx, E4M3, lo, lo + CHUNK)
+                nc.vector.tensor_tensor(
+                    out=ds_woven[:, LANES * c * CHUNK : LANES * (c + 1) * CHUNK].rearrange("p (c i t) -> p c t i", i=RUN, t=LANES),
+                    in0=bank[:].rearrange("p t (c i) -> p c t i", i=RUN),
+                    in1=slopes[:, :, lo : lo + CHUNK].rearrange("p t (c i) -> p c t i", i=RUN),
+                    op=ALU.mult,
+                )
+            quantize(qm_dealt, 2 * P * h, 2 * P, qm_mx, E4M3, 2 * P * h)
+            quantize(ds_woven, 0, HALF, ds_mx, E5M2, h * HALF)
+            for j in (1, 0):
+                first_banks[j, h] = gradient(j, h * HALF, (h + 1) * HALF, 2 * h + j)
+
+        out_planes = out_0.rearrange("(p j) t -> p j t", j=LANES)
+
+        def store(j):
+            nc.sync.dma_start(out=out_planes[:, j, :], in_=windows[j][:])
+
+        for h in range(2):
+            grads = [emptied(first_banks[j, h], "grad%d_%d" % (j, h)) for j in (1, 0)]
+            scalar_scatter(1, h * HALF, grads[0][:])
+            vector_scatter(0, h * HALF, grads[1][:])
+        store(1)
+        store(0)
+        bank3 = gradient(3, 0, N, 4)
+        grad3 = keep.tile([P, HALF], F32, name="grad3_0", tag="k_first", align_bytes=64)
+        nc.vector.tensor_copy(out=grad3[:], in_=bank3[:, :HALF])
+        vector_scatter(3, 0, grad3[:])
+        grad2 = emptied(gradient(2, 0, N, 5), "grad2")
+        late = keep.tile([P, HALF], F32, name="grad3_1")
+        nc.scalar.copy(out=late[:], in_=bank3[:, HALF:])
+        scalar_scatter(2, 0, grad2[:, :HALF])
+        scalar_scatter(3, HALF, late[:])
+        store(3)
+        scalar_scatter(2, HALF, grad2[:, HALF:])
+        store(2)
+        pairs = keep.tile([P, 2 * T * 2], BF16, name="pairs", tag="k_first", align_bytes=64)
         halves = pairs[:].rearrange("p (u n e) -> p u n e", u=2, e=2)
         pair_words = pairs[:].bitcast(F32).rearrange("p (u n) -> p u n", u=2)
-        cut = VECTOR_ROUNDS
-        out_planes = out_0.rearrange("(p j) t -> p j t", j=LANES)
-        for j in range(LANES):
-            for lo, hi in ((0, HALF), (HALF, N)) if j == 0 else ((0, N),):
-                nc.vector.tensor_copy(out=windows[j][:].indirect(offsets[:, lo // 16 : hi // 16]), in_=grads[j][:, lo:hi])
-            nc.sync.dma_start(out=out_planes[:, j, :], in_=windows[j][:])
-            if j < 2:
-                nc.scalar.copy(out=halves[:, 0, :, j], in_=windows[j][:])
-            elif j == 2:
-                nc.scalar.copy(out=halves[:, 1, :cut, 0], in_=windows[j][:, :cut])
-                nc.scalar.copy(out=halves[:, 1, cut:VECTOR_JOINS, 0], in_=windows[j][:, cut:VECTOR_JOINS])
-                nc.scalar.copy(
-                    out=halves[:, 1, :cut, :].rearrange("p (h n) e -> p h n e", h=2)[:, :, :LINK, :],
-                    in_=windows[j][:, :cut].rearrange("p (h n) -> p h n", h=2)[:, :, :LINK].unsqueeze(3).to_broadcast([P, 2, LINK, 2]),
-                )
-                nc.scalar.copy(out=halves[:, 1, VECTOR_JOINS:, 0], in_=windows[j][:, VECTOR_JOINS:])
-            else:
-                for lo, hi in ((0, cut // 2), (cut // 2, cut)):
-                    nc.vector.tensor_copy(out=halves[:, 1, lo:hi, 1], in_=windows[j][:, lo:hi])
-                for lo, hi in ((cut, VECTOR_JOINS), (VECTOR_JOINS, T - 2 * STEP), (T - 2 * STEP, T)):
-                    nc.scalar.copy(out=halves[:, 1, lo:hi, 1], in_=windows[j][:, lo:hi])
+        for j in (1, 0, 3):
+            nc.vector.tensor_copy(out=halves[:, j // 2, :, j % 2], in_=windows[j][:])
+        for lo, hi in ((0, 256), (256, 768), (768, 1280), (1280, T)):
+            nc.vector.tensor_copy(out=halves[:, 1, lo:hi, 0], in_=windows[2][:, lo:hi])
 
         out_scales = keep.tile([P, SPAN], U8, name="out_scales", align_bytes=64)
         out_words = out_1[0].rearrange("p t l -> p (t l)").bitcast(I32)
         out_codes = keep.tile([P, T], U32, name="out_codes", align_bytes=64)
         woven = {}
 
-        def join(first):
-            piece = keep.tile([P, STEP * LANES], BF16, name="woven" + str(first), align_bytes=64)
-            woven[first] = piece
-            for lo, hi, engine_copy in (
-                (first, min(first + STEP, VECTOR_JOINS), nc.vector.tensor_copy),
-                (max(first, VECTOR_JOINS), min(first + STEP, T - STEP // 2), nc.scalar.copy),
-                (max(first, T - STEP // 2), first + STEP, nc.scalar.copy),
-            ):
-                if lo < hi:
-                    dst = piece[:].bitcast(F32)[:, 2 * (lo - first) : 2 * (hi - first)].rearrange("p (g i u) -> p g u i", i=RUN, u=2)
-                    src = pair_words[:, :, lo:hi].rearrange("p u (g i) -> p g u i", i=RUN)
-                    engine_copy(out=dst, in_=src)
+        def weave(lo, engine_copy):
+            hi = lo + STEP
+            piece = keep.tile([P, STEP * LANES], BF16, name="woven" + str(lo), align_bytes=64)
+            woven[lo] = piece
+            dst = piece[:].bitcast(F32).rearrange("p (g i u) -> p g u i", i=RUN, u=2)
+            engine_copy(out=dst, in_=pair_words[:, :, lo:hi].rearrange("p u (g i) -> p g u i", i=RUN))
 
-        join(0)
-        for lo in range(0, T, STEP):
-            if lo + STEP < T:
-                join(lo + STEP)
+        def planes(lo):
             row, col = 4 * (lo // SPAN), lo % SPAN
-            width = STEP if lo + STEP < T else STEP // 2
-            for at in range(0, STEP, width):
-                nc.vector.quantize_mx(
-                    out=out_codes[:, lo + at : lo + at + width].bitcast(E4M3),
-                    scales=out_scales[row:P, col + at : col + at + width],
-                    in_=woven[lo][:, LANES * at : LANES * (at + width)],
-                )
-                last = lo + at + width
-                if last in STORE_ENDS:
-                    first = max([0] + [end for end in STORE_ENDS if end < last])
-                    nc.sync.dma_start(out=out_words[:, first:last], in_=out_codes[:, first:last].bitcast(I32))
+            nc.vector.quantize_mx(
+                out=out_codes[:, lo : lo + STEP].bitcast(E4M3),
+                scales=out_scales[row:P, col : col + STEP],
+                in_=woven[lo][:],
+            )
+
+        def store_codes(lo, hi):
+            nc.sync.dma_start(out=out_words[:, lo:hi], in_=out_codes[:, lo:hi].bitcast(I32))
+
+        for lo in (0, 256, 512, 1024, 768, 1536, 1280):
+            weave(lo, nc.scalar.copy)
+        weave(T - STEP, nc.vector.tensor_copy)
+        planes(0)
+        planes(256)
+        store_codes(0, 512)
+        planes(512)
+        planes(1792)
+        planes(1024)
+        planes(768)
+        store_codes(512, 1280)
+        planes(1536)
+        store_codes(1536, 2048)
+        planes(1280)
+        store_codes(1280, 1536)
         for quad in range(4):
             queue = nc.scalar if quad % 2 else nc.sync
             queue.dma_start(

@@ -22,7 +22,10 @@ HALF = N // 2
 CHUNK = 128
 RUN = 4
 DO_DEAL_SPLITS = (36, 30)
+POOL_FROM = 1024
+SCALAR_FROM = 512
 STEP = 256
+STORE_ENDS = (768, 1280, 1792, 2048)
 SPAN = 512
 
 
@@ -162,7 +165,7 @@ def tile_attend_gat_pl_tnh_k_kernel(tc, qT, kT, vT, doT, rw, qm, offs, out_0, ou
             return bank
 
         def emptied(bank, name):
-            grad = keep.tile([P, bank.shape[1]], F32, name=name)
+            grad = keep.tile([P, bank.shape[1]], F32, name=name, tag=name, align_bytes=64)
             nc.scalar.copy(out=grad[:], in_=bank[:])
             return grad
 
@@ -203,24 +206,33 @@ def tile_attend_gat_pl_tnh_k_kernel(tc, qT, kT, vT, doT, rw, qm, offs, out_0, ou
         store(1)
         store(0)
         bank3 = gradient(3, 0, N, 4)
-        grad3 = keep.tile([P, HALF], F32, name="grad3_0", tag="k_first", align_bytes=64)
-        nc.vector.tensor_copy(out=grad3[:], in_=bank3[:, :HALF])
-        vector_scatter(3, 0, grad3[:])
+        grad3 = keep.tile([P, N], F32, name="grad3", tag="k_first", align_bytes=64)
+        nc.vector.tensor_copy(out=grad3[:], in_=bank3[:])
         grad2 = emptied(gradient(2, 0, N, 5), "grad2")
-        late = keep.tile([P, HALF], F32, name="grad3_1")
-        nc.scalar.copy(out=late[:], in_=bank3[:, HALF:])
-        scalar_scatter(2, 0, grad2[:, :HALF])
-        scalar_scatter(3, HALF, late[:])
+        nc.vector.tensor_copy(out=windows[3][:].indirect(offsets[:]), in_=grad3[:])
         store(3)
-        scalar_scatter(2, HALF, grad2[:, HALF:])
-        store(2)
-        pairs = keep.tile([P, 2 * T * 2], BF16, name="pairs", tag="k_first", align_bytes=64)
-        halves = pairs[:].rearrange("p (u n e) -> p u n e", u=2, e=2)
-        pair_words = pairs[:].bitcast(F32).rearrange("p (u n) -> p u n", u=2)
-        for j in (1, 0, 3):
-            nc.vector.tensor_copy(out=halves[:, j // 2, :, j % 2], in_=windows[j][:])
-        for lo, hi in ((0, 256), (256, 768), (768, 1280), (1280, T)):
-            nc.vector.tensor_copy(out=halves[:, 1, lo:hi, 0], in_=windows[2][:, lo:hi])
+        for lo in (0, HALF):
+            scalar_scatter(2, lo, grad2[:, lo : lo + HALF])
+        nc.scalar.dma_start(out=out_planes[:, 2, :], in_=windows[2][:])
+
+        def pair_tile(name, tag, tokens):
+            pairs = keep.tile([P, 2 * tokens * 2], BF16, name=name, tag=tag, align_bytes=64)
+            return pairs[:].rearrange("p (u n e) -> p u n e", u=2, e=2), pairs[:].bitcast(F32).rearrange("p (u n) -> p u n", u=2)
+
+        early, early_words = pair_tile("early", "k_first", SCALAR_FROM)
+        middle, middle_words = pair_tile("middle", "grad2", POOL_FROM - SCALAR_FROM)
+        late, late_words = pair_tile("late", "late", T - POOL_FROM)
+        for j in (1, 0):
+            nc.gpsimd.tensor_scalar(out=late[:, 0, :, j], in0=windows[j][:, POOL_FROM:], scalar1=1.0, scalar2=0.0, op0=ALU.mult, op1=ALU.add)
+        for j in (2, 3):
+            nc.scalar.copy(out=middle[:, 1, :, j - 2], in_=windows[j][:, SCALAR_FROM:POOL_FROM])
+        for j in (1, 0, 3, 2):
+            nc.vector.tensor_copy(out=early[:, j // 2, :, j % 2], in_=windows[j][:, :SCALAR_FROM])
+        for j in (1, 0):
+            nc.vector.tensor_copy(out=middle[:, 0, :, j], in_=windows[j][:, SCALAR_FROM:POOL_FROM])
+        for j in (3, 2):
+            nc.vector.tensor_copy(out=late[:, 1, :, j - 2], in_=windows[j][:, POOL_FROM:])
+        pair_words = ((0, early_words), (SCALAR_FROM, middle_words), (POOL_FROM, late_words))
 
         out_scales = keep.tile([P, SPAN], U8, name="out_scales", align_bytes=64)
         out_words = out_1[0].rearrange("p t l -> p (t l)").bitcast(I32)
@@ -232,7 +244,8 @@ def tile_attend_gat_pl_tnh_k_kernel(tc, qT, kT, vT, doT, rw, qm, offs, out_0, ou
             piece = keep.tile([P, STEP * LANES], BF16, name="woven" + str(lo), align_bytes=64)
             woven[lo] = piece
             dst = piece[:].bitcast(F32).rearrange("p (g i u) -> p g u i", i=RUN, u=2)
-            engine_copy(out=dst, in_=pair_words[:, :, lo:hi].rearrange("p u (g i) -> p g u i", i=RUN))
+            first, words = [entry for entry in pair_words if entry[0] <= lo][-1]
+            engine_copy(out=dst, in_=words[:, :, lo - first : hi - first].rearrange("p u (g i) -> p g u i", i=RUN))
 
         def planes(lo):
             row, col = 4 * (lo // SPAN), lo % SPAN
@@ -245,21 +258,11 @@ def tile_attend_gat_pl_tnh_k_kernel(tc, qT, kT, vT, doT, rw, qm, offs, out_0, ou
         def store_codes(lo, hi):
             nc.sync.dma_start(out=out_words[:, lo:hi], in_=out_codes[:, lo:hi].bitcast(I32))
 
-        for lo in (0, 256, 512, 1024, 768, 1536, 1280):
+        for lo in range(0, T, STEP):
             weave(lo, nc.scalar.copy)
-        weave(T - STEP, nc.vector.tensor_copy)
-        planes(0)
-        planes(256)
-        store_codes(0, 512)
-        planes(512)
-        planes(1792)
-        planes(1024)
-        planes(768)
-        store_codes(512, 1280)
-        planes(1536)
-        store_codes(1536, 2048)
-        planes(1280)
-        store_codes(1280, 1536)
+            planes(lo)
+            if lo + STEP in STORE_ENDS:
+                store_codes(max([0] + [end for end in STORE_ENDS if end <= lo]), lo + STEP)
         for quad in range(4):
             queue = nc.scalar if quad % 2 else nc.sync
             queue.dma_start(

@@ -58,8 +58,8 @@ def tile_attend_gat_pl_tnh_k_kernel(tc, qT, kT, vT, doT, rw, qm, offs, out_0, ou
             dst = dealt[:].rearrange("p (t g h j) -> p g j h t", t=LANES, h=2, j=LANES)[:, 32 * h : 32 * h + 32]
             return dst, raw[:].rearrange("p j (g h t) -> p g j h t", h=2, t=LANES)
 
-        def mx_tiles(name, width):
-            codes = keep.tile([P, width], U32, name=name + "_codes", align_bytes=64)
+        def mx_tiles(name, width, codes_tag=""):
+            codes = keep.tile([P, width], U32, name=name + "_codes", tag=codes_tag or name + "_codes", align_bytes=64)
             scales = keep.tile([P, width], U8, name=name + "_scales", align_bytes=64)
             return codes, scales
 
@@ -68,7 +68,7 @@ def tile_attend_gat_pl_tnh_k_kernel(tc, qT, kT, vT, doT, rw, qm, offs, out_0, ou
             nc.scalar.copy(out=dst[:, split:], in_=src[:, split:])
 
         def deal_views(raw, name):
-            dealt = keep.tile([P, LANES * 512], BF16, name=name, align_bytes=64)
+            dealt = keep.tile([P, LANES * 512], BF16, name=name, tag=name, align_bytes=64)
             dst = dealt[:].rearrange("p (t g h j) -> p g j h t", t=LANES, h=2, j=LANES)
             src = raw[:].rearrange("p j (g h t) -> p g j h t", h=2, t=LANES)
             return dealt, dst, src
@@ -141,9 +141,8 @@ def tile_attend_gat_pl_tnh_k_kernel(tc, qT, kT, vT, doT, rw, qm, offs, out_0, ou
         for j in range(LANES):
             for lo, hi in ((0, N),) if j < LANES - 1 else ((0, HALF), (HALF, N)):
                 nc.vector.tensor_copy(out=v_lanes[:, lo:hi, j], in_=v_planes[j][:].indirect(listed(lo, hi)))
-        v_mx = mx_tiles("v", N)
-        for lo in (0, HALF):
-            quantize(v_woven, lo, HALF, v_mx, E4M3, lo)
+        v_mx = [mx_tiles("v0", HALF)]
+        quantize(v_woven, 0, HALF, v_mx[0], E4M3, 0)
         do_mx = mx_tiles("do", R)
         do_dealt, dst, src = deal_views(do_raw, "do_dealt")
         for pair, split in enumerate(DO_DEAL_SPLITS):
@@ -151,6 +150,8 @@ def tile_attend_gat_pl_tnh_k_kernel(tc, qT, kT, vT, doT, rw, qm, offs, out_0, ou
             shared_copy(dst[:, :, :, :, tiles], src[:, :, :, :, tiles], split)
         for first in (0, 2 * P):
             quantize(do_dealt, first, 2 * P, do_mx, E5M2, first)
+        v_mx.append(mx_tiles("v1", HALF, "do_dealt"))
+        quantize(v_woven, HALF, HALF, v_mx[1], E4M3, 0)
         qm_dealt = keep.tile([P, LANES * D], BF16, name="qm_dealt", align_bytes=64)
         for h, tiles in ((0, slice(0, LANES)), (1, slice(0, 2)), (1, slice(2, LANES))):
             dst, src = half_views(qm_dealt, qm_raw[h], h)
@@ -182,17 +183,28 @@ def tile_attend_gat_pl_tnh_k_kernel(tc, qT, kT, vT, doT, rw, qm, offs, out_0, ou
                 lo = h * HALF + c * CHUNK
                 bank = psum.tile([P, LANES, CHUNK], F32, name="dp" + str(lo), tag="bank" + str(LANES + lo // CHUNK))
                 for t in range(LANES):
-                    product(bank[:, t, :], do_mx, E5M2, t, v_mx, E4M3, lo, lo + CHUNK)
+                    product(bank[:, t, :], do_mx, E5M2, t, v_mx[h], E4M3, c * CHUNK, (c + 1) * CHUNK)
                 nc.vector.tensor_tensor(
                     out=ds_woven[:, LANES * c * CHUNK : LANES * (c + 1) * CHUNK].rearrange("p (c i t) -> p c t i", i=RUN, t=LANES),
                     in0=bank[:].rearrange("p t (c i) -> p c t i", i=RUN),
                     in1=slopes[:, :, lo : lo + CHUNK].rearrange("p t (c i) -> p c t i", i=RUN),
                     op=ALU.mult,
                 )
-            quantize(qm_dealt, 2 * P * h, 2 * P, qm_mx, E4M3, 2 * P * h)
-            quantize(ds_woven, 0, HALF, ds_mx, E5M2, h * HALF)
-            for j in (1, 0):
-                first_banks[j, h] = gradient(j, h * HALF, (h + 1) * HALF, 2 * h + j)
+            if h == 0:
+                bank = psum.tile([P, HALF], F32, name="dk1_0", tag="bank1")
+                quantize(ds_woven, 0, CHUNK, ds_mx, E5M2, 0)
+                quantize(qm_dealt, P, P, qm_mx, E4M3, P)
+                product(bank[:, :CHUNK], qm_mx, E4M3, 1, ds_mx, E5M2, 0, CHUNK)
+                quantize(ds_woven, CHUNK, CHUNK, ds_mx, E5M2, CHUNK)
+                product(bank[:, CHUNK:], qm_mx, E4M3, 1, ds_mx, E5M2, CHUNK, HALF)
+                quantize(qm_dealt, 0, P, qm_mx, E4M3, 0)
+                first_banks[1, 0] = bank
+                first_banks[0, 0] = gradient(0, 0, HALF, 0)
+            else:
+                quantize(qm_dealt, 2 * P, 2 * P, qm_mx, E4M3, 2 * P)
+                quantize(ds_woven, 0, HALF, ds_mx, E5M2, HALF)
+                for j in (1, 0):
+                    first_banks[j, 1] = gradient(j, HALF, N, 2 + j)
 
         out_planes = out_0.rearrange("(p j) t -> p j t", j=LANES)
 
@@ -237,32 +249,30 @@ def tile_attend_gat_pl_tnh_k_kernel(tc, qT, kT, vT, doT, rw, qm, offs, out_0, ou
         out_scales = keep.tile([P, SPAN], U8, name="out_scales", align_bytes=64)
         out_words = out_1[0].rearrange("p t l -> p (t l)").bitcast(I32)
         out_codes = keep.tile([P, T], U32, name="out_codes", align_bytes=64)
-        woven = {}
 
-        def weave(lo, engine_copy):
-            hi = lo + STEP
-            piece = keep.tile([P, STEP * LANES], BF16, name="woven" + str(lo), align_bytes=64)
-            woven[lo] = piece
-            dst = piece[:].bitcast(F32).rearrange("p (g i u) -> p g u i", i=RUN, u=2)
+        def weave(lo, hi):
+            piece = keep.tile([P, (hi - lo) * LANES], BF16, name="woven" + str(lo), align_bytes=64)
             first, words = [entry for entry in pair_words if entry[0] <= lo][-1]
-            engine_copy(out=dst, in_=words[:, :, lo - first : hi - first].rearrange("p u (g i) -> p g u i", i=RUN))
+            dst = piece[:].bitcast(F32).rearrange("p (g i u) -> p g u i", i=RUN, u=2)
+            nc.scalar.copy(out=dst, in_=words[:, :, lo - first : hi - first].rearrange("p u (g i) -> p g u i", i=RUN))
+            return piece
 
-        def planes(lo):
+        def planes(piece, lo, hi):
             row, col = 4 * (lo // SPAN), lo % SPAN
             nc.vector.quantize_mx(
-                out=out_codes[:, lo : lo + STEP].bitcast(E4M3),
-                scales=out_scales[row:P, col : col + STEP],
-                in_=woven[lo][:],
+                out=out_codes[:, lo:hi].bitcast(E4M3),
+                scales=out_scales[row:P, col : col + hi - lo],
+                in_=piece[:],
             )
 
         def store_codes(lo, hi):
             nc.sync.dma_start(out=out_words[:, lo:hi], in_=out_codes[:, lo:hi].bitcast(I32))
 
-        for lo in range(0, T, STEP):
-            weave(lo, nc.scalar.copy)
-            planes(lo)
-            if lo + STEP in STORE_ENDS:
-                store_codes(max([0] + [end for end in STORE_ENDS if end <= lo]), lo + STEP)
+        starts = list(range(0, T, STEP)) + [T - STEP // 2, T]
+        for lo, hi in zip(starts, starts[1:]):
+            planes(weave(lo, hi), lo, hi)
+            if hi in STORE_ENDS:
+                store_codes(max([0] + [end for end in STORE_ENDS if end < hi]), hi)
         for quad in range(4):
             queue = nc.scalar if quad % 2 else nc.sync
             queue.dma_start(

@@ -23,7 +23,7 @@ CHUNK = 128
 RUN = 4
 DO_DEAL_SPLITS = (36, 30)
 POOL_FROM = 1024
-SCALAR_FROM = 512
+SCALAR_FROM = 768
 STEP = 256
 STORE_ENDS = (768, 1280, 1792, 2048)
 SPAN = 512

@@ -97,9 +97,7 @@ def tile_attend_gat_pl_tnh_k_kernel(tc, qT, kT, vT, doT, rw, qm, offs, out_0, ou
         nc.sync.dma_start(offsets[:], offs)
         gate = keep.tile([P, LANES], F32, name="gate")
         nc.scalar.dma_start(out=gate[:], in_=rw[0].rearrange("(p j) o -> p (j o)", j=LANES))
-        k_first = keep.tile([P, 2, T], F32, name="k_first", tag="k_first", align_bytes=64)
-        nc.sync.dma_start(out=k_first[:], in_=kT.rearrange("(p j) t -> p j t", j=LANES)[:, :2, :])
-        k_planes = [k_first[:, 0, :], k_first[:, 1, :]] + [load_plane(kT, j, "kpool")[:] for j in (2, 3)]
+        k_planes = [load_plane(kT, j, "kpool") for j in range(LANES)]
         v_planes = [load_plane(vT, j, "vpool") for j in range(LANES)]
         do_raw = load_square(doT, "do_raw")
         qm_raw = load_halves(qm, "qm_raw")
@@ -121,7 +119,7 @@ def tile_attend_gat_pl_tnh_k_kernel(tc, qT, kT, vT, doT, rw, qm, offs, out_0, ou
         k_woven = keep.tile([P, N * LANES], BF16, name="k_woven", tag="k_woven", align_bytes=64)
         k_lanes = k_woven[:].rearrange("p (n j) -> p n j", j=LANES)
         for j in range(LANES):
-            nc.vector.tensor_copy(out=k_lanes[:, :, j], in_=k_planes[j].indirect(offsets[:]))
+            nc.vector.tensor_copy(out=k_lanes[:, :, j], in_=k_planes[j][:].indirect(offsets[:]))
         k_mx = mx_tiles("k", N)
         quantize(k_woven, 0, N, k_mx, E4M3, 0)
         negated = keep.tile([P, LANES], F32, name="negated")
@@ -218,7 +216,7 @@ def tile_attend_gat_pl_tnh_k_kernel(tc, qT, kT, vT, doT, rw, qm, offs, out_0, ou
         store(1)
         store(0)
         bank3 = gradient(3, 0, N, 4)
-        grad3 = keep.tile([P, N], F32, name="grad3", tag="k_first", align_bytes=64)
+        grad3 = keep.tile([P, N], F32, name="grad3", tag="grad3", align_bytes=64)
         nc.vector.tensor_copy(out=grad3[:], in_=bank3[:])
         grad2 = emptied(gradient(2, 0, N, 5), "grad2")
         nc.vector.tensor_copy(out=windows[3][:].indirect(offsets[:]), in_=grad3[:])
@@ -231,7 +229,7 @@ def tile_attend_gat_pl_tnh_k_kernel(tc, qT, kT, vT, doT, rw, qm, offs, out_0, ou
             pairs = keep.tile([P, 2 * tokens * 2], BF16, name=name, tag=tag, align_bytes=64)
             return pairs[:].rearrange("p (u n e) -> p u n e", u=2, e=2), pairs[:].bitcast(F32).rearrange("p (u n) -> p u n", u=2)
 
-        early, early_words = pair_tile("early", "k_first", SCALAR_FROM)
+        early, early_words = pair_tile("early", "grad3", SCALAR_FROM)
         middle, middle_words = pair_tile("middle", "grad2", POOL_FROM - SCALAR_FROM)
         late, late_words = pair_tile("late", "late", T - POOL_FROM)
         for j in (1, 0):

@@ -21,7 +21,7 @@ LANES = 4
 HALF = N // 2
 CHUNK = 128
 RUN = 4
-DO_DEAL_SPLITS = (36, 30)
+DO_DEAL_SPLITS = (42, 32)
 POOL_FROM = 1024
 SCALAR_FROM = 768
 STEP = 256
@@ -183,9 +183,9 @@ def tile_attend_gat_pl_tnh_k_kernel(tc, qT, kT, vT, doT, rw, qm, offs, out_0, ou
                 for t in range(LANES):
                     product(bank[:, t, :], do_mx, E5M2, t, v_mx[h], E4M3, c * CHUNK, (c + 1) * CHUNK)
                 nc.vector.tensor_tensor(
-                    out=ds_woven[:, LANES * c * CHUNK : LANES * (c + 1) * CHUNK].rearrange("p (c i t) -> p c t i", i=RUN, t=LANES),
-                    in0=bank[:].rearrange("p t (c i) -> p c t i", i=RUN),
-                    in1=slopes[:, :, lo : lo + CHUNK].rearrange("p t (c i) -> p c t i", i=RUN),
+                    out=ds_woven[:, LANES * c * CHUNK : LANES * (c + 1) * CHUNK].rearrange("p (c i t) -> p c t i", i=2, t=LANES),
+                    in0=bank[:].rearrange("p t (c i) -> p c t i", i=2),
+                    in1=slopes[:, :, lo : lo + CHUNK].rearrange("p t (c i) -> p c t i", i=2),
                     op=ALU.mult,
                 )
             if h == 0:

@@ -23,7 +23,7 @@ CHUNK = 128
 RUN = 4
 DO_DEAL_SPLITS = (42, 32)
 POOL_FROM = 1024
-SCALAR_FROM = 768
+SCALAR_TOKENS = 256
 STEP = 256
 STORE_ENDS = (768, 1280, 1792, 2048)
 SPAN = 512
@@ -218,31 +218,40 @@ def tile_attend_gat_pl_tnh_k_kernel(tc, qT, kT, vT, doT, rw, qm, offs, out_0, ou
         bank3 = gradient(3, 0, N, 4)
         grad3 = keep.tile([P, N], F32, name="grad3", tag="grad3", align_bytes=64)
         nc.vector.tensor_copy(out=grad3[:], in_=bank3[:])
-        grad2 = emptied(gradient(2, 0, N, 5), "grad2")
         nc.vector.tensor_copy(out=windows[3][:].indirect(offsets[:]), in_=grad3[:])
         store(3)
-        for lo in (0, HALF):
-            scalar_scatter(2, lo, grad2[:, lo : lo + HALF])
-        nc.scalar.dma_start(out=out_planes[:, 2, :], in_=windows[2][:])
 
         def pair_tile(name, tag, tokens):
             pairs = keep.tile([P, 2 * tokens * 2], BF16, name=name, tag=tag, align_bytes=64)
             return pairs[:].rearrange("p (u n e) -> p u n e", u=2, e=2), pairs[:].bitcast(F32).rearrange("p (u n) -> p u n", u=2)
 
-        early, early_words = pair_tile("early", "grad3", SCALAR_FROM)
-        middle, middle_words = pair_tile("middle", "grad2", POOL_FROM - SCALAR_FROM)
+        early, early_words = pair_tile("early", "early", SCALAR_TOKENS)
+        middle, middle_words = pair_tile("middle", "grad3", POOL_FROM - SCALAR_TOKENS)
         late, late_words = pair_tile("late", "late", T - POOL_FROM)
+
+        def scalar_round(j):
+            nc.scalar.copy(out=early[:, j // 2, :, j % 2], in_=windows[j][:, :SCALAR_TOKENS])
+
+        bank2 = gradient(2, 0, N, 5)
+        grad2 = keep.tile([P, N], F32, name="grad2")
+        for lo in (0, HALF):
+            nc.scalar.copy(out=grad2[:, lo : lo + HALF], in_=bank2[:, lo : lo + HALF])
+        for lo, j in ((0, 1), (HALF, 0)):
+            scalar_scatter(2, lo, grad2[:, lo : lo + HALF])
+            scalar_round(j)
+        nc.scalar.dma_start(out=out_planes[:, 2, :], in_=windows[2][:])
+        for j in (2, 3):
+            scalar_round(j)
+
         for j in (1, 0):
             nc.gpsimd.tensor_scalar(out=late[:, 0, :, j], in0=windows[j][:, POOL_FROM:], scalar1=1.0, scalar2=0.0, op0=ALU.mult, op1=ALU.add)
-        for j in (2, 3):
-            nc.scalar.copy(out=middle[:, 1, :, j - 2], in_=windows[j][:, SCALAR_FROM:POOL_FROM])
-        for j in (1, 0, 3, 2):
-            nc.vector.tensor_copy(out=early[:, j // 2, :, j % 2], in_=windows[j][:, :SCALAR_FROM])
-        for j in (1, 0):
-            nc.vector.tensor_copy(out=middle[:, 0, :, j], in_=windows[j][:, SCALAR_FROM:POOL_FROM])
-        for j in (3, 2):
-            nc.vector.tensor_copy(out=late[:, 1, :, j - 2], in_=windows[j][:, POOL_FROM:])
-        pair_words = ((0, early_words), (SCALAR_FROM, middle_words), (POOL_FROM, late_words))
+        for lo, hi in ((SCALAR_TOKENS, SPAN), (SPAN, POOL_FROM)):
+            for j in (1, 0, 3, 2):
+                nc.vector.tensor_copy(out=middle[:, j // 2, lo - SCALAR_TOKENS : hi - SCALAR_TOKENS, j % 2], in_=windows[j][:, lo:hi])
+        for lo in range(POOL_FROM, T, SPAN):
+            for j in (3, 2):
+                nc.vector.tensor_copy(out=late[:, 1, lo - POOL_FROM : lo + SPAN - POOL_FROM, j - 2], in_=windows[j][:, lo : lo + SPAN])
+        pair_words = ((0, early_words), (SCALAR_TOKENS, middle_words), (POOL_FROM, late_words))
 
         out_scales = keep.tile([P, SPAN], U8, name="out_scales", align_bytes=64)
         out_words = out_1[0].rearrange("p t l -> p (t l)").bitcast(I32)

@@ -24,6 +24,7 @@ RUN = 4
 DO_DEAL_SPLITS = (42, 32)
 POOL_FROM = 1024
 SCALAR_TOKENS = 256
+QM_PARTS = ((0, 384), (384, 512))
 STEP = 256
 STORE_ENDS = (768, 1280, 1792, 2048)
 SPAN = 512
@@ -45,17 +46,18 @@ def tile_attend_gat_pl_tnh_k_kernel(tc, qT, kT, vT, doT, rw, qm, offs, out_0, ou
             nc.sync.dma_start(out=raw[:], in_=src[0].rearrange("(p j) w -> p j w", j=LANES))
             return raw
 
-        def load_halves(src, name):
+        def load_parts(src, name):
             rows = src[0].rearrange("(p j) w -> p j w", j=LANES)
             raws = []
-            for h in range(2):
-                raw = keep.tile([P, LANES, 256], F32, name=name + str(h), align_bytes=64)
-                nc.sync.dma_start(out=raw[:], in_=rows[:, :, 256 * h : 256 * (h + 1)])
+            for lo, hi in QM_PARTS:
+                raw = keep.tile([P, LANES, hi - lo], F32, name=name + str(lo), align_bytes=64)
+                nc.sync.dma_start(out=raw[:], in_=rows[:, :, lo:hi])
                 raws.append(raw)
             return raws
 
-        def half_views(dealt, raw, h):
-            dst = dealt[:].rearrange("p (t g h j) -> p g j h t", t=LANES, h=2, j=LANES)[:, 32 * h : 32 * h + 32]
+        def part_views(dealt, raw, part):
+            lo, hi = QM_PARTS[part]
+            dst = dealt[:].rearrange("p (t g h j) -> p g j h t", t=LANES, h=2, j=LANES)[:, lo // 8 : hi // 8]
             return dst, raw[:].rearrange("p j (g h t) -> p g j h t", h=2, t=LANES)
 
         def mx_tiles(name, width, codes_tag=""):
@@ -100,7 +102,7 @@ def tile_attend_gat_pl_tnh_k_kernel(tc, qT, kT, vT, doT, rw, qm, offs, out_0, ou
         k_planes = [load_plane(kT, j, "kpool") for j in range(LANES)]
         v_planes = [load_plane(vT, j, "vpool") for j in range(LANES)]
         do_raw = load_square(doT, "do_raw")
-        qm_raw = load_halves(qm, "qm_raw")
+        qm_raw = load_parts(qm, "qm_raw")
 
         def listed(lo, hi):
             return offsets[:, lo // 16 : hi // 16]
@@ -139,21 +141,23 @@ def tile_attend_gat_pl_tnh_k_kernel(tc, qT, kT, vT, doT, rw, qm, offs, out_0, ou
         for j in range(LANES):
             for lo, hi in ((0, N),) if j < LANES - 1 else ((0, HALF), (HALF, N)):
                 nc.vector.tensor_copy(out=v_lanes[:, lo:hi, j], in_=v_planes[j][:].indirect(listed(lo, hi)))
-        v_mx = [mx_tiles("v0", HALF)]
-        quantize(v_woven, 0, HALF, v_mx[0], E4M3, 0)
+        v_first = mx_tiles("v_first", CHUNK)
+        quantize(v_woven, 0, CHUNK, v_first, E4M3, 0)
         do_mx = mx_tiles("do", R)
         do_dealt, dst, src = deal_views(do_raw, "do_dealt")
         for pair, split in enumerate(DO_DEAL_SPLITS):
             tiles = slice(2 * pair, 2 * pair + 2)
             shared_copy(dst[:, :, :, :, tiles], src[:, :, :, :, tiles], split)
-        for first in (0, 2 * P):
-            quantize(do_dealt, first, 2 * P, do_mx, E5M2, first)
-        v_mx.append(mx_tiles("v1", HALF, "do_dealt"))
-        quantize(v_woven, HALF, HALF, v_mx[1], E4M3, 0)
+        for first, count in ((0, 2 * P), (2 * P, P), (3 * P, P)):
+            quantize(do_dealt, first, count, do_mx, E5M2, first)
+        v_rest = mx_tiles("v_rest", N - CHUNK, "do_dealt")
+        quantize(v_woven, CHUNK, CHUNK, v_rest, E4M3, 0)
+        quantize(v_woven, HALF, HALF, v_rest, E4M3, CHUNK)
         qm_dealt = keep.tile([P, LANES * D], BF16, name="qm_dealt", align_bytes=64)
-        for h, tiles in ((0, slice(0, LANES)), (1, slice(0, 2)), (1, slice(2, LANES))):
-            dst, src = half_views(qm_dealt, qm_raw[h], h)
-            nc.scalar.copy(out=dst[:, :, :, :, tiles], in_=src[:, :, :, :, tiles])
+        for tiles in (slice(0, 2), slice(2, LANES)):
+            for part in range(2):
+                dst, src = part_views(qm_dealt, qm_raw[part], part)
+                nc.scalar.copy(out=dst[:, :, :, :, tiles], in_=src[:, :, :, :, tiles])
 
         ds_mx = mx_tiles("ds", N)
         qm_mx = mx_tiles("qm", D)
@@ -181,7 +185,7 @@ def tile_attend_gat_pl_tnh_k_kernel(tc, qT, kT, vT, doT, rw, qm, offs, out_0, ou
                 lo = h * HALF + c * CHUNK
                 bank = psum.tile([P, LANES, CHUNK], F32, name="dp" + str(lo), tag="bank" + str(LANES + lo // CHUNK))
                 for t in range(LANES):
-                    product(bank[:, t, :], do_mx, E5M2, t, v_mx[h], E4M3, c * CHUNK, (c + 1) * CHUNK)
+                    product(bank[:, t, :], do_mx, E5M2, t, v_rest if lo else v_first, E4M3, max(lo - CHUNK, 0), max(lo, CHUNK))
                 nc.vector.tensor_tensor(
                     out=ds_woven[:, LANES * c * CHUNK : LANES * (c + 1) * CHUNK].rearrange("p (c i t) -> p c t i", i=2, t=LANES),
                     in0=bank[:].rearrange("p t (c i) -> p c t i", i=2),
@@ -217,7 +221,8 @@ def tile_attend_gat_pl_tnh_k_kernel(tc, qT, kT, vT, doT, rw, qm, offs, out_0, ou
         store(0)
         bank3 = gradient(3, 0, N, 4)
         grad3 = keep.tile([P, N], F32, name="grad3", tag="grad3", align_bytes=64)
-        nc.vector.tensor_copy(out=grad3[:], in_=bank3[:])
+        nc.vector.tensor_copy(out=grad3[:, :HALF], in_=bank3[:, :HALF])
+        nc.scalar.copy(out=grad3[:, HALF:], in_=bank3[:, HALF:])
         nc.vector.tensor_copy(out=windows[3][:].indirect(offsets[:]), in_=grad3[:])
         store(3)
 

@@ -25,6 +25,7 @@ DO_DEAL_SPLITS = (42, 32)
 POOL_FROM = 1024
 SCALAR_TOKENS = 256
 QM_PARTS = ((0, 384), (384, 512))
+FILL_TOKENS = 128
 STEP = 256
 STORE_ENDS = (768, 1280, 1792, 2048)
 SPAN = 512
@@ -193,14 +194,13 @@ def tile_attend_gat_pl_tnh_k_kernel(tc, qT, kT, vT, doT, rw, qm, offs, out_0, ou
                     op=ALU.mult,
                 )
             if h == 0:
-                bank = psum.tile([P, HALF], F32, name="dk1_0", tag="bank1")
+                first_grad = keep.tile([P, HALF], F32, name="grad1_0")
                 quantize(ds_woven, 0, CHUNK, ds_mx, E5M2, 0)
                 quantize(qm_dealt, P, P, qm_mx, E4M3, P)
-                product(bank[:, :CHUNK], qm_mx, E4M3, 1, ds_mx, E5M2, 0, CHUNK)
+                nc.scalar.copy(out=first_grad[:, :CHUNK], in_=gradient(1, 0, CHUNK, 1)[:])
                 quantize(ds_woven, CHUNK, CHUNK, ds_mx, E5M2, CHUNK)
-                product(bank[:, CHUNK:], qm_mx, E4M3, 1, ds_mx, E5M2, CHUNK, HALF)
+                nc.scalar.copy(out=first_grad[:, CHUNK:], in_=gradient(1, CHUNK, HALF, 4)[:])
                 quantize(qm_dealt, 0, P, qm_mx, E4M3, 0)
-                first_banks[1, 0] = bank
                 first_banks[0, 0] = gradient(0, 0, HALF, 0)
             else:
                 quantize(qm_dealt, 2 * P, 2 * P, qm_mx, E4M3, 2 * P)
@@ -214,15 +214,14 @@ def tile_attend_gat_pl_tnh_k_kernel(tc, qT, kT, vT, doT, rw, qm, offs, out_0, ou
             nc.sync.dma_start(out=out_planes[:, j, :], in_=windows[j][:])
 
         for h in range(2):
-            grads = [emptied(first_banks[j, h], "grad%d_%d" % (j, h)) for j in (1, 0)]
+            grads = [first_grad if (j, h) == (1, 0) else emptied(first_banks[j, h], "grad%d_%d" % (j, h)) for j in (1, 0)]
             scalar_scatter(1, h * HALF, grads[0][:])
             vector_scatter(0, h * HALF, grads[1][:])
         store(1)
         store(0)
         bank3 = gradient(3, 0, N, 4)
         grad3 = keep.tile([P, N], F32, name="grad3", tag="grad3", align_bytes=64)
-        nc.vector.tensor_copy(out=grad3[:, :HALF], in_=bank3[:, :HALF])
-        nc.scalar.copy(out=grad3[:, HALF:], in_=bank3[:, HALF:])
+        nc.vector.tensor_copy(out=grad3[:], in_=bank3[:])
         nc.vector.tensor_copy(out=windows[3][:].indirect(offsets[:]), in_=grad3[:])
         store(3)
 
@@ -234,8 +233,8 @@ def tile_attend_gat_pl_tnh_k_kernel(tc, qT, kT, vT, doT, rw, qm, offs, out_0, ou
         middle, middle_words = pair_tile("middle", "grad3", POOL_FROM - SCALAR_TOKENS)
         late, late_words = pair_tile("late", "late", T - POOL_FROM)
 
-        def scalar_round(j):
-            nc.scalar.copy(out=early[:, j // 2, :, j % 2], in_=windows[j][:, :SCALAR_TOKENS])
+        def scalar_round(j, lo, hi):
+            nc.scalar.copy(out=early[:, j // 2, lo:hi, j % 2], in_=windows[j][:, lo:hi])
 
         bank2 = gradient(2, 0, N, 5)
         grad2 = keep.tile([P, N], F32, name="grad2")
@@ -243,10 +242,12 @@ def tile_attend_gat_pl_tnh_k_kernel(tc, qT, kT, vT, doT, rw, qm, offs, out_0, ou
             nc.scalar.copy(out=grad2[:, lo : lo + HALF], in_=bank2[:, lo : lo + HALF])
         for lo, j in ((0, 1), (HALF, 0)):
             scalar_scatter(2, lo, grad2[:, lo : lo + HALF])
-            scalar_round(j)
+            scalar_round(j, 0, FILL_TOKENS)
         nc.scalar.dma_start(out=out_planes[:, 2, :], in_=windows[2][:])
+        for j in (1, 0):
+            scalar_round(j, FILL_TOKENS, SCALAR_TOKENS)
         for j in (2, 3):
-            scalar_round(j)
+            scalar_round(j, 0, SCALAR_TOKENS)
 
         for j in (1, 0):
             nc.gpsimd.tensor_scalar(out=late[:, 0, :, j], in0=windows[j][:, POOL_FROM:], scalar1=1.0, scalar2=0.0, op0=ALU.mult, op1=ALU.add)

@@ -22,7 +22,7 @@ HALF = N // 2
 CHUNK = 128
 RUN = 4
 DO_DEAL_SPLITS = (42, 32)
-POOL_FROM = 1024
+POOL_FROM = 896
 SCALAR_TOKENS = 256
 QM_PARTS = ((0, 384), (384, 512))
 FILL_TOKENS = 128
@@ -254,9 +254,9 @@ def tile_attend_gat_pl_tnh_k_kernel(tc, qT, kT, vT, doT, rw, qm, offs, out_0, ou
         for lo, hi in ((SCALAR_TOKENS, SPAN), (SPAN, POOL_FROM)):
             for j in (1, 0, 3, 2):
                 nc.vector.tensor_copy(out=middle[:, j // 2, lo - SCALAR_TOKENS : hi - SCALAR_TOKENS, j % 2], in_=windows[j][:, lo:hi])
-        for lo in range(POOL_FROM, T, SPAN):
+        for lo, hi in ((POOL_FROM, T - SPAN), (T - SPAN, T)):
             for j in (3, 2):
-                nc.vector.tensor_copy(out=late[:, 1, lo - POOL_FROM : lo + SPAN - POOL_FROM, j - 2], in_=windows[j][:, lo : lo + SPAN])
+                nc.vector.tensor_copy(out=late[:, 1, lo - POOL_FROM : hi - POOL_FROM, j - 2], in_=windows[j][:, lo:hi])
         pair_words = ((0, early_words), (SCALAR_TOKENS, middle_words), (POOL_FROM, late_words))
 
         out_scales = keep.tile([P, SPAN], U8, name="out_scales", align_bytes=64)
@@ -281,7 +281,7 @@ def tile_attend_gat_pl_tnh_k_kernel(tc, qT, kT, vT, doT, rw, qm, offs, out_0, ou
         def store_codes(lo, hi):
             nc.sync.dma_start(out=out_words[:, lo:hi], in_=out_codes[:, lo:hi].bitcast(I32))
 
-        starts = list(range(0, T, STEP)) + [T - STEP // 2, T]
+        starts = sorted(set(range(0, T, STEP)) | {POOL_FROM, T - STEP // 2, T})
         for lo, hi in zip(starts, starts[1:]):
             planes(weave(lo, hi), lo, hi)
             if hi in STORE_ENDS:

@@ -24,6 +24,7 @@ RUN = 4
 DO_DEAL_SPLITS = (42, 32)
 POOL_FROM = 896
 SCALAR_TOKENS = 256
+SCALAR_LOW_TOKENS = 384
 QM_PARTS = ((0, 384), (384, 512))
 FILL_TOKENS = 128
 STEP = 256
@@ -248,12 +249,15 @@ def tile_attend_gat_pl_tnh_k_kernel(tc, qT, kT, vT, doT, rw, qm, offs, out_0, ou
             scalar_round(j, FILL_TOKENS, SCALAR_TOKENS)
         for j in (2, 3):
             scalar_round(j, 0, SCALAR_TOKENS)
+        for j in (1, 0):
+            nc.scalar.copy(out=middle[:, 0, : SCALAR_LOW_TOKENS - SCALAR_TOKENS, j], in_=windows[j][:, SCALAR_TOKENS:SCALAR_LOW_TOKENS])
 
         for j in (1, 0):
             nc.gpsimd.tensor_scalar(out=late[:, 0, :, j], in0=windows[j][:, POOL_FROM:], scalar1=1.0, scalar2=0.0, op0=ALU.mult, op1=ALU.add)
         for lo, hi in ((SCALAR_TOKENS, SPAN), (SPAN, POOL_FROM)):
-            for j in (1, 0, 3, 2):
-                nc.vector.tensor_copy(out=middle[:, j // 2, lo - SCALAR_TOKENS : hi - SCALAR_TOKENS, j % 2], in_=windows[j][:, lo:hi])
+            for j in (3, 2, 1, 0):
+                start = max(lo, SCALAR_LOW_TOKENS) if j < 2 else lo
+                nc.vector.tensor_copy(out=middle[:, j // 2, start - SCALAR_TOKENS : hi - SCALAR_TOKENS, j % 2], in_=windows[j][:, start:hi])
         for lo, hi in ((POOL_FROM, T - SPAN), (T - SPAN, T)):
             for j in (3, 2):
                 nc.vector.tensor_copy(out=late[:, 1, lo - POOL_FROM : hi - POOL_FROM, j - 2], in_=windows[j][:, lo:hi])

@@ -25,6 +25,7 @@ DO_DEAL_SPLITS = (42, 32)
 POOL_FROM = 896
 SCALAR_TOKENS = 256
 SCALAR_LOW_TOKENS = 384
+KEY_SPLIT = 320
 QM_PARTS = ((0, 384), (384, 512))
 FILL_TOKENS = 128
 STEP = 256
@@ -122,8 +123,13 @@ def tile_attend_gat_pl_tnh_k_kernel(tc, qT, kT, vT, doT, rw, qm, offs, out_0, ou
         quantize(q_dealt, 0, R, q_mx, E4M3, 0)
         k_woven = keep.tile([P, N * LANES], BF16, name="k_woven", tag="k_woven", align_bytes=64)
         k_lanes = k_woven[:].rearrange("p (n j) -> p n j", j=LANES)
+        k_pair = keep.tile([P, 2, N - KEY_SPLIT], BF16, name="k_pair", align_bytes=64)
         for j in range(LANES):
-            nc.vector.tensor_copy(out=k_lanes[:, :, j], in_=k_planes[j][:].indirect(offsets[:]))
+            hi = N if j < 2 else KEY_SPLIT
+            nc.vector.tensor_copy(out=k_lanes[:, :hi, j], in_=k_planes[j][:].indirect(listed(0, hi)))
+            if hi < N:
+                nc.scalar.activation(out=k_pair[:, j - 2, :], in_=k_planes[j][:].indirect(listed(hi, N)), func=ACT.Copy)
+        nc.scalar.copy(out=k_lanes[:, KEY_SPLIT:, 2:], in_=k_pair[:].rearrange("p e n -> p n e"))
         k_mx = mx_tiles("k", N)
         quantize(k_woven, 0, N, k_mx, E4M3, 0)
         negated = keep.tile([P, LANES], F32, name="negated")

@@ -142,7 +142,7 @@ def tile_attend_gat_pl_tnh_k_kernel(tc, qT, kT, vT, doT, rw, qm, offs, out_0, ou
             nc.scalar.activation(out=weight[:], in_=bank[:], func=ACT.Tanh)
             square = keep.tile([P, N], F32, name="square" + str(t))
             nc.scalar.activation(out=square[:], in_=weight[:], func=ACT.Square)
-            nc.scalar.activation(out=slopes[:, t, :], in_=square[:], func=ACT.Identity, scale=negated[:, t : t + 1], bias=gate[:, t : t + 1])
+            nc.gpsimd.tensor_scalar(out=slopes[:, t, :], in0=square[:], scalar1=negated[:, t : t + 1], scalar2=gate[:, t : t + 1], op0=ALU.mult, op1=ALU.add)
 
         v_woven = keep.tile([P, N * LANES], BF16, name="v_woven", tag="k_woven", align_bytes=64)
         v_lanes = v_woven[:].rearrange("p (n j) -> p n j", j=LANES)

from contextlib import ExitStack

import concourse.mybir as mybir

N, T, D, DV, R = 512, 2048, 512, 512, 512
FLOPS = 2 * N * R * (D + DV + D)

F32 = mybir.dt.float32
BF16 = mybir.dt.bfloat16
I32 = mybir.dt.int32
U32 = mybir.dt.uint32
U16 = mybir.dt.uint16
U8 = mybir.dt.uint8
E4M3 = mybir.dt.float8_e4m3fn_x4
E5M2 = mybir.dt.float8_e5m2_x4
ACT = mybir.ActivationFunctionType
ALU = mybir.AluOpType

P = 128
LANES = 4
HALF = N // 2
CHUNK = 128
RUN = 4
DO_DEAL_SPLITS = (42, 32)
POOL_FROM = 896
SCALAR_TOKENS = 256
SCALAR_LOW_TOKENS = 384
KEY_SPLIT = 320
QM_PARTS = ((0, 384), (384, 512))
FILL_TOKENS = 128
STEP = 256
STORE_ENDS = (768, 1280, 1792, 2048)
SPAN = 512


def tile_attend_gat_pl_tnh_k_kernel(tc, qT, kT, vT, doT, rw, qm, offs, out_0, out_1, out_2):
    nc = tc.nc
    with ExitStack() as ctx:
        keep = ctx.enter_context(tc.tile_pool(name="keep", bufs=1))
        psum = ctx.enter_context(tc.psum_pool(name="psum", bufs=1))

        def load_plane(src, j, tag):
            plane = keep.tile([P, T], F32, name=tag + str(j), align_bytes=64)
            nc.sync.dma_start(out=plane[:], in_=src.rearrange("(p j) t -> p j t", j=LANES)[:, j, :])
            return plane

        def load_square(src, name):
            raw = keep.tile([P, LANES, 512], F32, name=name, align_bytes=64)
            nc.sync.dma_start(out=raw[:], in_=src[0].rearrange("(p j) w -> p j w", j=LANES))
            return raw

        def load_parts(src, name):
            rows = src[0].rearrange("(p j) w -> p j w", j=LANES)
            raws = []
            for lo, hi in QM_PARTS:
                raw = keep.tile([P, LANES, hi - lo], F32, name=name + str(lo), align_bytes=64)
                nc.sync.dma_start(out=raw[:], in_=rows[:, :, lo:hi])
                raws.append(raw)
            return raws

        def part_views(dealt, raw, part):
            lo, hi = QM_PARTS[part]
            dst = dealt[:].rearrange("p (t g h j) -> p g j h t", t=LANES, h=2, j=LANES)[:, lo // 8 : hi // 8]
            return dst, raw[:].rearrange("p j (g h t) -> p g j h t", h=2, t=LANES)

        def mx_tiles(name, width, codes_tag=""):
            codes = keep.tile([P, width], U32, name=name + "_codes", tag=codes_tag or name + "_codes", align_bytes=64)
            scales = keep.tile([P, width], U8, name=name + "_scales", align_bytes=64)
            return codes, scales

        def shared_copy(dst, src, split):
            nc.vector.tensor_copy(out=dst[:, :split], in_=src[:, :split])
            nc.scalar.copy(out=dst[:, split:], in_=src[:, split:])

        def deal_views(raw, name):
            dealt = keep.tile([P, LANES * 512], BF16, name=name, tag=name, align_bytes=64)
            dst = dealt[:].rearrange("p (t g h j) -> p g j h t", t=LANES, h=2, j=LANES)
            src = raw[:].rearrange("p j (g h t) -> p g j h t", h=2, t=LANES)
            return dealt, dst, src

        def quantize(src, first, count, mx, fmt, at):
            nc.vector.quantize_mx(
                out=mx[0][:, at : at + count].bitcast(fmt),
                scales=mx[1][:, at : at + count],
                in_=src[:, LANES * first : LANES * (first + count)],
            )

        def product(out, stat, stat_fmt, tile, mov, mov_fmt, lo, hi):
            cols = slice(tile * P, (tile + 1) * P)
            nc.tensor.matmul_mx(
                out=out,
                lhsT=stat[0][:, cols].bitcast(stat_fmt),
                lhsT_scale=stat[1][:, cols],
                rhs=mov[0][:, lo:hi].bitcast(mov_fmt),
                rhs_scale=mov[1][:, lo:hi],
                start=True,
                stop=True,
            )

        q_raw = load_square(qT, "q_raw")
        offsets = keep.tile([P, N // 16], U16, name="offsets")
        nc.sync.dma_start(offsets[:], offs)
        gate = keep.tile([P, LANES], F32, name="gate")
        nc.scalar.dma_start(out=gate[:], in_=rw[0].rearrange("(p j) o -> p (j o)", j=LANES))
        k_planes = [load_plane(kT, j, "kpool") for j in range(LANES)]
        v_planes = [load_plane(vT, j, "vpool") for j in range(LANES)]
        do_raw = load_square(doT, "do_raw")
        qm_raw = load_parts(qm, "qm_raw")

        def listed(lo, hi):
            return offsets[:, lo // 16 : hi // 16]

        windows = []
        for j in range(LANES):
            window = keep.tile([P, T], F32, name="window" + str(j), align_bytes=64)
            engine = nc.vector if j < 2 else nc.gpsimd
            engine.memset(window[:].bitcast(I32), 0)
            windows.append(window)

        q_mx = mx_tiles("q", R)
        q_dealt, dst, src = deal_views(q_raw, "q_dealt")
        nc.scalar.copy(out=dst, in_=src)
        quantize(q_dealt, 0, R, q_mx, E4M3, 0)
        k_woven = keep.tile([P, N * LANES], BF16, name="k_woven", tag="k_woven", align_bytes=64)
        k_lanes = k_woven[:].rearrange("p (n j) -> p n j", j=LANES)
        k_pair = keep.tile([P, 2, N - KEY_SPLIT], BF16, name="k_pair", align_bytes=64)
        for j in range(LANES):
            hi = N if j < 2 else KEY_SPLIT
            nc.vector.tensor_copy(out=k_lanes[:, :hi, j], in_=k_planes[j][:].indirect(listed(0, hi)))
            if hi < N:
                nc.scalar.activation(out=k_pair[:, j - 2, :], in_=k_planes[j][:].indirect(listed(hi, N)), func=ACT.Copy)
        nc.scalar.copy(out=k_lanes[:, KEY_SPLIT:, 2:], in_=k_pair[:].rearrange("p e n -> p n e"))
        k_mx = mx_tiles("k", N)
        quantize(k_woven, 0, N, k_mx, E4M3, 0)
        negated = keep.tile([P, LANES], F32, name="negated")
        nc.scalar.activation(out=negated[:], in_=gate[:], func=ACT.Copy, scale=-1.0)
        slopes = keep.tile([P, LANES, N], F32, name="slopes", align_bytes=64)
        for t in range(LANES):
            bank = psum.tile([P, N], F32, name="score" + str(t), tag="bank" + str(t))
            product(bank[:], q_mx, E4M3, t, k_mx, E4M3, 0, N)
            weight = keep.tile([P, N], F32, name="weight" + str(t))
            nc.scalar.activation(out=weight[:], in_=bank[:], func=ACT.Tanh)
            square = keep.tile([P, N], F32, name="square" + str(t))
            nc.scalar.activation(out=square[:], in_=weight[:], func=ACT.Square)
            nc.gpsimd.tensor_scalar(out=slopes[:, t, :], in0=square[:], scalar1=negated[:, t : t + 1], scalar2=gate[:, t : t + 1], op0=ALU.mult, op1=ALU.add)

        v_woven = keep.tile([P, N * LANES], BF16, name="v_woven", tag="k_woven", align_bytes=64)
        v_lanes = v_woven[:].rearrange("p (n j) -> p n j", j=LANES)
        for j in range(LANES):
            for lo, hi in ((0, N),) if j < LANES - 1 else ((0, HALF), (HALF, N)):
                nc.vector.tensor_copy(out=v_lanes[:, lo:hi, j], in_=v_planes[j][:].indirect(listed(lo, hi)))
        v_first = mx_tiles("v_first", CHUNK)
        quantize(v_woven, 0, CHUNK, v_first, E4M3, 0)
        do_mx = mx_tiles("do", R)
        do_dealt, dst, src = deal_views(do_raw, "do_dealt")
        for pair, split in enumerate(DO_DEAL_SPLITS):
            tiles = slice(2 * pair, 2 * pair + 2)
            shared_copy(dst[:, :, :, :, tiles], src[:, :, :, :, tiles], split)
        for first, count in ((0, 2 * P), (2 * P, P), (3 * P, P)):
            quantize(do_dealt, first, count, do_mx, E5M2, first)
        v_rest = mx_tiles("v_rest", N - CHUNK, "do_dealt")
        quantize(v_woven, CHUNK, CHUNK, v_rest, E4M3, 0)
        quantize(v_woven, HALF, HALF, v_rest, E4M3, CHUNK)
        qm_dealt = keep.tile([P, LANES * D], BF16, name="qm_dealt", align_bytes=64)
        for tiles in (slice(0, 2), slice(2, LANES)):
            for part in range(2):
                dst, src = part_views(qm_dealt, qm_raw[part], part)
                nc.scalar.copy(out=dst[:, :, :, :, tiles], in_=src[:, :, :, :, tiles])

        ds_mx = mx_tiles("ds", N)
        qm_mx = mx_tiles("qm", D)

        def gradient(j, lo, hi, bank_number):
            bank = psum.tile([P, hi - lo], F32, name="dk%d_%d" % (j, lo), tag="bank" + str(bank_number))
            product(bank[:], qm_mx, E4M3, j, ds_mx, E5M2, lo, hi)
            return bank

        def emptied(bank, name):
            grad = keep.tile([P, bank.shape[1]], F32, name=name, tag=name, align_bytes=64)
            nc.scalar.copy(out=grad[:], in_=bank[:])
            return grad

        def vector_scatter(j, lo, values):
            nc.vector.tensor_copy(out=windows[j][:].indirect(listed(lo, lo + HALF)), in_=values)

        def scalar_scatter(j, lo, values):
            nc.scalar.activation(out=windows[j][:].indirect(listed(lo, lo + HALF)), in_=values, func=ACT.Copy)

        first_banks = {}
        for h in range(2):
            ds_woven = keep.tile([P, HALF * LANES], BF16, name="ds_woven" + str(h), align_bytes=64)
            for c in range(2):
                lo = h * HALF + c * CHUNK
                bank = psum.tile([P, LANES, CHUNK], F32, name="dp" + str(lo), tag="bank" + str(LANES + lo // CHUNK))
                for t in range(LANES):
                    product(bank[:, t, :], do_mx, E5M2, t, v_rest if lo else v_first, E4M3, max(lo - CHUNK, 0), max(lo, CHUNK))
                nc.vector.tensor_tensor(
                    out=ds_woven[:, LANES * c * CHUNK : LANES * (c + 1) * CHUNK].rearrange("p (c i t) -> p c t i", i=2, t=LANES),
                    in0=bank[:].rearrange("p t (c i) -> p c t i", i=2),
                    in1=slopes[:, :, lo : lo + CHUNK].rearrange("p t (c i) -> p c t i", i=2),
                    op=ALU.mult,
                )
            if h == 0:
                first_grad = keep.tile([P, HALF], F32, name="grad1_0")
                quantize(ds_woven, 0, CHUNK, ds_mx, E5M2, 0)
                quantize(qm_dealt, P, P, qm_mx, E4M3, P)
                nc.scalar.copy(out=first_grad[:, :CHUNK], in_=gradient(1, 0, CHUNK, 1)[:])
                quantize(ds_woven, CHUNK, CHUNK, ds_mx, E5M2, CHUNK)
                nc.scalar.copy(out=first_grad[:, CHUNK:], in_=gradient(1, CHUNK, HALF, 4)[:])
                quantize(qm_dealt, 0, P, qm_mx, E4M3, 0)
                first_banks[0, 0] = gradient(0, 0, HALF, 0)
            else:
                quantize(qm_dealt, 2 * P, 2 * P, qm_mx, E4M3, 2 * P)
                quantize(ds_woven, 0, HALF, ds_mx, E5M2, HALF)
                for j in (1, 0):
                    first_banks[j, 1] = gradient(j, HALF, N, 2 + j)

        out_planes = out_0.rearrange("(p j) t -> p j t", j=LANES)

        def store(j):
            nc.sync.dma_start(out=out_planes[:, j, :], in_=windows[j][:])

        for h in range(2):
            grads = [first_grad if (j, h) == (1, 0) else emptied(first_banks[j, h], "grad%d_%d" % (j, h)) for j in (1, 0)]
            scalar_scatter(1, h * HALF, grads[0][:])
            vector_scatter(0, h * HALF, grads[1][:])
        store(1)
        store(0)
        bank3 = gradient(3, 0, N, 4)
        grad3 = keep.tile([P, N], F32, name="grad3", tag="grad3", align_bytes=64)
        nc.vector.tensor_copy(out=grad3[:], in_=bank3[:])
        nc.vector.tensor_copy(out=windows[3][:].indirect(offsets[:]), in_=grad3[:])
        store(3)

        def pair_tile(name, tag, tokens):
            pairs = keep.tile([P, 2 * tokens * 2], BF16, name=name, tag=tag, align_bytes=64)
            return pairs[:].rearrange("p (u n e) -> p u n e", u=2, e=2), pairs[:].bitcast(F32).rearrange("p (u n) -> p u n", u=2)

        early, early_words = pair_tile("early", "early", SCALAR_TOKENS)
        middle, middle_words = pair_tile("middle", "grad3", POOL_FROM - SCALAR_TOKENS)
        late, late_words = pair_tile("late", "late", T - POOL_FROM)

        def scalar_round(j, lo, hi):
            nc.scalar.copy(out=early[:, j // 2, lo:hi, j % 2], in_=windows[j][:, lo:hi])

        bank2 = gradient(2, 0, N, 5)
        grad2 = keep.tile([P, N], F32, name="grad2")
        for lo in (0, HALF):
            nc.scalar.copy(out=grad2[:, lo : lo + HALF], in_=bank2[:, lo : lo + HALF])
        for lo, j in ((0, 1), (HALF, 0)):
            scalar_scatter(2, lo, grad2[:, lo : lo + HALF])
            scalar_round(j, 0, FILL_TOKENS)
        nc.scalar.dma_start(out=out_planes[:, 2, :], in_=windows[2][:])
        for j in (1, 0):
            scalar_round(j, FILL_TOKENS, SCALAR_TOKENS)
        for j in (2, 3):
            scalar_round(j, 0, SCALAR_TOKENS)
        for j in (1, 0):
            nc.scalar.copy(out=middle[:, 0, : SCALAR_LOW_TOKENS - SCALAR_TOKENS, j], in_=windows[j][:, SCALAR_TOKENS:SCALAR_LOW_TOKENS])

        for j in (1, 0):
            nc.gpsimd.tensor_scalar(out=late[:, 0, :, j], in0=windows[j][:, POOL_FROM:], scalar1=1.0, scalar2=0.0, op0=ALU.mult, op1=ALU.add)
        for lo, hi in ((SCALAR_TOKENS, SPAN), (SPAN, POOL_FROM)):
            for j in (3, 2, 1, 0):
                start = max(lo, SCALAR_LOW_TOKENS) if j < 2 else lo
                nc.vector.tensor_copy(out=middle[:, j // 2, start - SCALAR_TOKENS : hi - SCALAR_TOKENS, j % 2], in_=windows[j][:, start:hi])
        for lo, hi in ((POOL_FROM, T - SPAN), (T - SPAN, T)):
            for j in (3, 2):
                nc.vector.tensor_copy(out=late[:, 1, lo - POOL_FROM : hi - POOL_FROM, j - 2], in_=windows[j][:, lo:hi])
        pair_words = ((0, early_words), (SCALAR_TOKENS, middle_words), (POOL_FROM, late_words))

        out_scales = keep.tile([P, SPAN], U8, name="out_scales", align_bytes=64)
        out_words = out_1[0].rearrange("p t l -> p (t l)").bitcast(I32)
        out_codes = keep.tile([P, T], U32, name="out_codes", align_bytes=64)

        def weave(lo, hi):
            piece = keep.tile([P, (hi - lo) * LANES], BF16, name="woven" + str(lo), align_bytes=64)
            first, words = [entry for entry in pair_words if entry[0] <= lo][-1]
            dst = piece[:].bitcast(F32).rearrange("p (g i u) -> p g u i", i=RUN, u=2)
            nc.scalar.copy(out=dst, in_=words[:, :, lo - first : hi - first].rearrange("p u (g i) -> p g u i", i=RUN))
            return piece

        def planes(piece, lo, hi):
            row, col = 4 * (lo // SPAN), lo % SPAN
            nc.vector.quantize_mx(
                out=out_codes[:, lo:hi].bitcast(E4M3),
                scales=out_scales[row:P, col : col + hi - lo],
                in_=piece[:],
            )

        def store_codes(lo, hi):
            nc.sync.dma_start(out=out_words[:, lo:hi], in_=out_codes[:, lo:hi].bitcast(I32))

        starts = sorted(set(range(0, T, STEP)) | {POOL_FROM, T - STEP // 2, T})
        for lo, hi in zip(starts, starts[1:]):
            planes(weave(lo, hi), lo, hi)
            if hi in STORE_ENDS:
                store_codes(max([0] + [end for end in STORE_ENDS if end < hi]), hi)
        for quad in range(4):
            queue = nc.scalar if quad % 2 else nc.sync
            queue.dma_start(
                out=out_2[0, 4 * quad : 4 * quad + 4, :].bitcast(I32).rearrange("i (s x) -> s i x", s=T // SPAN),
                in_=out_scales[32 * quad : 32 * quad + 16, :].bitcast(I32),
            )
